import numpy as np, ml_dtypes
CORES = [2,6,10,14,18,22,26,30]
N = 8
BF = ml_dtypes.bfloat16
def gentries(a):
    return np.ascontiguousarray(a.reshape(8, 16, -1).transpose(0, 2, 1)).reshape(8, -1)
def gtable(e):
    e = np.asarray(e); return np.ascontiguousarray(e.reshape(8, -1, 16).transpose(0, 2, 1)).reshape(128, -1).astype(np.int32)
R, F, C, D, B = 16384, 4096, 512, 1, 1 << 20
def passing(at, lim):
    a0 = at[:, 0].reshape(8, R); l = lim.reshape(8, 2)
    return (a0 >= l[:, :1]) & (a0 <= l[:, 1:])
def dims(rng, m, w, first=None):
    lo = rng.integers(-(B >> 1), B >> 2, (8, 1)); hi = lo + w[:, None]; z = rng.random((8, R))
    if first is not None: z[np.arange(8), first] = -1
    ok = np.argsort(np.argsort(z, 1), 1) < m[:, None]
    out = np.where(rng.random((8, R)) < 0.5, rng.integers(1 - B, lo, (8, R)), rng.integers(hi + 1, B, (8, R)))
    return lo, hi, ok, np.where(ok, rng.integers(lo, hi + 1, (8, R)), out)
def living(n, z):
    return np.argsort(np.argsort(z, 1), 1) < n[:, None]
def facts(rng, ok, live, p, where, e=1):
    m = np.sum(ok, axis=1)[:, None]; o = np.argsort(~ok, 1, kind="stable")
    bad = rng.random((N, 8, F)) < p; np.put_along_axis(bad, where, True, 1); bad = bad & ~live[:, None]
    k = np.where(bad, R - m, m); j = np.minimum((rng.random((N, 8, F)) ** e * k).astype(np.int64), k - 1)
    return o[np.arange(8)[:, None], j + np.where(bad, m, 0)]
def pack(lo, hi, v, rest, fk, me):
    rest[:, 0] = v
    return {"at": np.ascontiguousarray(rest.reshape(N, D, 16, R).transpose(0, 2, 1, 3)).reshape(N, 16, D * R).astype(np.int32),
            "lim": np.concatenate([lo, hi], 1).reshape(N, 1, 2 * D).astype(np.int32), "fk": np.stack([gtable(x) for x in fk]), "me": me.reshape(N, 1, F).astype(np.int32)}
def whole(rng, *shape):
    return rng.integers(1 - B, B, shape)
def setup_inputs(rng):
    lo, hi, ok, v = dims(rng, rng.integers(R // 4, 3 * R // 4, 8), rng.integers(B >> 6, B >> 2, 8))
    live = living(rng.integers(C // 4, C, N), rng.random((N, F)))
    return pack(lo, hi, v, whole(rng, 8, 16, R), facts(rng, ok, live, 0.15, rng.integers(0, 8, (N, 1, F))), whole(rng, N, F))
def setup_inputs_full(rng):
    lo, hi, ok, v = dims(rng, rng.integers(R // 4, 3 * R // 4, 8), rng.integers(B >> 6, B >> 2, 8))
    n = np.full(N, C); n[rng.integers(0, N)] = 1; z = rng.random((N, F)); z[:, 0] = -1; z[:, -1] = -2
    return pack(lo, hi, v, whole(rng, 8, 16, R), facts(rng, ok, living(n, z), 0.3, rng.integers(0, 8, (N, 1, F))), whole(rng, N, F))
def setup_inputs_ends(rng):
    w = np.where(rng.permutation(8) < 3, 0, rng.integers(1, 1000, 8))
    lo, hi, ok, v = dims(rng, rng.integers(R // 4, 3 * R // 4, 8), w); h = rng.random((8, R)) < 0.5
    v = np.where(ok, np.where(h, lo, hi), np.where(h, lo - 1, hi + 1)); j = np.arange(F)
    live = living(rng.integers(C // 4, C + 1, N), np.minimum(j, F - 1 - j)[None] + np.zeros((N, 1)))
    return pack(lo, hi, v, whole(rng, 8, 16, R), facts(rng, ok, live, 0.1, rng.integers(0, 8, (N, 1, F))), whole(rng, N, F))
def setup_inputs_alike(rng):
    m = np.where(rng.permutation(8) < 4, 1, R - 1)
    lo, hi, ok, v = dims(rng, m, rng.integers(0, B >> 2, 8), np.where(rng.random(8) < 0.5, 0, R - 1))
    live = living(rng.integers(C // 4, C + 1, N), rng.random((N, F))); fk = facts(rng, ok, live, 0.1, rng.integers(0, 8, (N, 1, F)))
    q = rng.integers(0, N); s = np.flatnonzero(live[q]); fk[q][:, s] = fk[q][:, s[:1]]
    return pack(lo, hi, v, whole(rng, 8, 16, R), fk, whole(rng, N, F))
def setup_inputs_near(rng):
    lo, hi, ok, v = dims(rng, rng.integers(R // 4, 3 * R // 4, 8), rng.integers(B >> 6, B >> 2, 8))
    where = np.where(rng.random((N, 1, 1)) < 0.5, rng.integers(0, 8, (N, 1, 1)), rng.integers(0, 8, (N, 1, F)))
    live = living(rng.integers(C // 4, C + 1, N), rng.random((N, F))); sg = rng.choice(np.array([-1, 1]), (1, 16, 1))
    rest = sg * (B - 1 - rng.integers(0, 50, (8, 16, R))); me = rng.choice(np.array([-1, 1]), (N, 1)) * (B - 1 - rng.integers(0, 50, (N, F)))
    return pack(lo, hi, v, rest, facts(rng, ok, live, 0.0, where), me)
def setup_inputs_spread(rng):
    lo, hi, ok, v = dims(rng, np.maximum(1, R >> rng.integers(1, 10, 8)), 1 << rng.integers(0, 18, 8))
    live = living(np.maximum(1, C >> rng.integers(0, 6, N)), rng.random((N, F)))
    rest = whole(rng, 8, 16, R) >> rng.integers(0, 20, (8, 16, R)); me = whole(rng, N, F) >> rng.integers(0, 20, (N, F))
    return pack(lo, hi, v, rest, facts(rng, ok, live, rng.random((1, 8, 1)), rng.integers(0, 8, (N, 1, F)), 4), me)
def check_inputs(d):
    bad = [k for k in ("at", "lim", "me") if not ((d[k] > -B) & (d[k] < B)).all()]
    if not ((d["fk"] >= 0) & (d["fk"] < R)).all(): return bad + ["fk"]
    ok = passing(d["at"], d["lim"]); g = np.arange(8)[:, None]
    n = [int(np.sum(np.all(ok[g, gentries(a)], axis=0))) for a in d["fk"]]
    return bad + ([] if min(n) >= 1 and max(n) <= C else ["survivors"])
def reference(at, lim, fk, me):
    y = np.zeros((N, 16, C + 1), np.int64); ok = passing(at, lim); g = np.arange(8)[:, None]
    a = np.ascontiguousarray(at.reshape(N, 16, D, R).transpose(0, 2, 1, 3)).reshape(8, 16, R).astype(np.int64)
    for r in range(N):
        k = gentries(fk[r]); s = np.flatnonzero(np.all(ok[g, k], axis=0)); n = len(s)
        y[r, :, :n] = me[r, 0][s][None]
        for d in range(8): y[r, :, :n] += a[d][:, k[d, s]]
        y[r, :, C] = n
    return {"y": np.asarray(y, np.float32)}

@@ -1,0 +1,415 @@
+import math
+from concourse.bass import DstId, RemoteDMATransfer
+from concourse.mybir import AluOpType as A, ActivationFunctionType as Fn
+
+F32, BF, I32, U16 = "float32", "bfloat16", "int32", "uint16"
+WIN = 5120
+HALF = 8192
+SCRATCH = {}
+for _t, _list in (
+        (BF, "f1 128,f2 128,pall 128,o1 128,onesb 128,zb 32,m16 16,gp 1,wp 16,wn 16,bd 128,sm 2048,idb 128,tri 128,qs 8,"
+             "bb 256,rb 256,vb 512,win8 2048,gw 4096,t0 64,t1 64,s0 32,s1 32,sv 32,cum 32,win 5120,sel 8,selh 8"),
+        (I32, "a0 128,im 16,im2 16,gi 1,ib 128,ib2 128,fks 256,wi 256,bi 256,u0 128,u1 128,v0 128,v1 128,sg 1,mn 512,"
+              "ml 32,ml2 32,at2 8200"),
+        (F32, "onesf 128,m16f 16,gf 1,gpf 1,xj 32,xj1 32,rt 256,e1 32,e2 32,e3 32,z 32,rx2 32,ax0 128,ax1 128,sgf 1,"
+              "ga 1024,sel2 64,zs 512,rx3 512,q1 256,q2 128,q3 64,prm 128,mv 512,mwin 5120,b7 112"),
+        (U16, "w16 256,off 32,off2 64,ml16 32")):
+    for _x in _list.split(","):
+        SCRATCH[_x.split()[0]] = ("sbuf", [128, int(_x.split()[1])], _t)
+SCRATCH["lm"] = ("sbuf", [1, 2], I32)
+SCRATCH["lf"] = ("sbuf", [1, 2], F32)
+SCRATCH["yo"] = ("sbuf", [64, 129], F32)
+for _k in ("lh", "ll"):
+    SCRATCH[_k] = ("sbuf", [64, 128], BF)
+for _k in ("vr", "vh", "vl"):
+    SCRATCH[_k] = ("sbuf", [64, 512], I32)
+for _k in ("hb", "lb"):
+    SCRATCH[_k] = ("sbuf", [64, 512], BF)
+for _k in range(8):
+    SCRATCH["p%d" % _k] = ("psum", [128, 512], F32)
+SEMAPHORES = ["x1", "x2", "x3", "l1", "l2", "l3"] + ["e%d" % k for k in range(130)]
+
+
+def distance_order(core, T, topo):
+    here = topo.chip(core)
+    chips = []
+    for c in T.cores:
+        if topo.chip(c) not in chips:
+            chips.append(topo.chip(c))
+
+    def far(ch):
+        if ch == here:
+            return 0
+        if topo.mates(ch, here):
+            return 1
+        return 2 if topo.same_plane(ch, here) else 3
+    out = []
+    for ch in sorted(chips, key=lambda ch: (-far(ch), (ch - here) % len(chips))):
+        out.append((ch, [r for r in range(len(T.cores)) if topo.chip(T.cores[r]) == ch]))
+    return out
+
+
+def plans(core, T, topo):
+    me = T.rank_of(core)
+    order = distance_order(core, T, topo)
+    far = [r for ch, rs in order[:-1] for r in rs]
+    near = [r for r in order[-1][1] if r != me]
+    eo = topo.engines(core, T.cores[far[0]])
+    en = [e for e in topo.engines(core, T.cores[near[0]]) if e not in eo]
+    x1 = [[(far, eo), (near, en[:2])]]
+    x2 = [[([far[k]], eo[2 * k:2 * k + 2]) for k in range(4)] + [(near, en[:2])],
+          [([far[4 + k]], eo[4 * k:4 * k + 4]) for k in range(2)]]
+    x3 = [[([far[2 * k]], eo[0:4]), ([far[2 * k + 1]], eo[4:8])] for k in range(3)] + [[(near, en[:4])]]
+    return order, x1, x2, x3
+
+
+def arriving(core, T, topo, which):
+    me, n = T.rank_of(core), 0
+    for c in T.cores:
+        if c != core:
+            for call in plans(c, T, topo)[which]:
+                for dests, eng in call:
+                    if me in dests:
+                        n += len(eng)
+    return n
+
+
+def rank_program(g, core, T, topo):
+    me = T.rank_of(core)
+    if me is None:
+        return
+    V, S, P, Y = g.vector, g.scalar, g.tensor, g.sync
+    names = {"g": g, "V": V, "S": S, "P": P, "Y": Y}
+    evs = []
+    known = {k: [] for k in names}
+    waited = []
+
+    def ev():
+        evs.append(0)
+        return len(evs) - 1
+
+    def inc(e, ins, n=1):
+        ins.then_inc(T.sem["e%d" % e], n)
+        evs[e] += n
+        return e
+
+    def one(ins, n=1):
+        return inc(ev(), ins, n)
+
+    def w(qn, *es):
+        for e in es:
+            if e not in known[qn]:
+                names[qn].wait_ge(T.sem["e%d" % e], evs[e])
+                known[qn].append(e)
+                waited.append(e)
+
+    def mm(out, lhsT, rhs, start=True, stop=True):
+        return P.matmul(out, lhsT, rhs, start, stop)
+
+    def copy(qn, out, in_):
+        return V.tensor_copy(out, in_) if qn == "V" else S.activation(out, in_, Fn.Copy)
+
+    order, x1, x2, x3 = plans(core, T, topo)
+    n1, n2, n3 = [arriving(core, T, topo, k) for k in (1, 2, 3)]
+
+    def send(calls, rsem, lsem, src, dst):
+        n = 0
+        for call in calls:
+            tr = []
+            for dests, eng in call:
+                ids = []
+                for r in dests:
+                    rid, pid, se = topo.addr(T.cores[r])
+                    ids.append(DstId(rid=rid, pnc=pid))
+                tr.append(RemoteDMATransfer(dst_ids=ids, dma_engine_mask=sum(1 << e for e in eng), remote_sem=rsem,
+                                            srcs=[src(dests[0])], dsts=[dst] * len(dests)))
+                n += len(eng)
+            g.remote_dma_fused(tr, local_sem=lsem)
+        return n
+
+    e_lim = one(S.dma_start(T.lm[:, :], T.lim[:, :]), 16)
+    e_a0 = one(Y.dma_start(T.a0[:, :], T["at"][0:1, :]), 16)
+    e_fk = one(S.dma_start(T.fks[:, :], T.fk[:, :]), 16)
+    e_vr = ev()
+    for k in range(8):
+        inc(e_vr, Y.dma_start(T.vr[8 * k:8 * k + 8, :], T.fk[:, 32 * k:32 * k + 32]), 16)
+
+    e_im = one(g.iota(T.im[:, :], [[-1, 16]], 0, 1))
+    e_onesb = one(V.memset(T.onesb[:, :], 1.0))
+    e_slot = ev()
+    inc(e_slot, V.memset(T.at2[:, 0:1], 0))
+    inc(e_slot, V.memset(T.at2[:, HALF + 1:HALF + 8], 0))
+    e_onesf = one(V.memset(T.onesf[:, :], 1.0))
+    e_ib = one(g.iota(T.ib[:, :], [[-16, 8], [0, 16]], 0, 1))
+    w("V", e_im)
+    e_gi = one(V.tensor_scalar(T.gi[:, :], T.im[:, 0:1], 4, None, A.arith_shift_right))
+    e_im2 = one(V.tensor_scalar(T.im2[:, :], T.im[:, :], 15, None, A.bitwise_and))
+    w("V", e_gi)
+    e_gf = one(V.tensor_copy(T.gf[:, :], T.gi[:, :]))
+    w("V", e_im2)
+    e_m16 = one(V.tensor_scalar(T.m16[:, :], T.im2[:, :], 0.0, None, A.is_equal))
+    w("S", e_gf)
+    e_gp = one(S.activation(T.gp[:, :], T.gf[:, :], Fn.Exp, scale=math.log(2.0)))
+    w("V", e_ib)
+    e_ib2 = one(V.tensor_scalar(T.ib2[:, :], T.ib[:, :], 4, None, A.arith_shift_right))
+    w("V", e_ib2)
+    e_bd = one(V.tensor_scalar(T.bd[:, :], T.ib2[:, :], 0.0, None, A.is_equal))
+    w("V", e_m16)
+    e_m16f = one(V.tensor_copy(T.m16f[:, :], T.m16[:, :]))
+    e_zb = one(V.memset(T.zb[:, :], 0.0))
+    w("V", e_bd, e_m16f)
+    e_sm = ev()
+    for m in range(16):
+        inc(e_sm, V.tensor_scalar(T.sm[:, 128 * m:128 * m + 128], T.bd[:, :], T.m16f[:, m:m + 1], None, A.mult))
+    w("V", e_gp)
+    e_gpf = one(V.tensor_copy(T.gpf[:, :], T.gp[:, :]))
+    w("V", e_gpf)
+    e_w = ev()
+    inc(e_w, V.tensor_scalar(T.wp[:, :], T.m16[:, :], T.gpf[:, 0:1], None, A.mult))
+    inc(e_w, V.tensor_scalar(T.wn[:, :], T.m16[:, :], T.gpf[:, 0:1], -1.0, A.mult, A.mult))
+    w("g", e_onesb)
+    e_id = one(g.affine_select(T.idb[:, :], T.onesb[:, :], [[-1, 128]], A.is_equal, 0.0, 0, 1))
+    e_tri = one(g.affine_select(T.tri[:, :], T.onesb[:, :], [[1, 128]], A.is_gt, 0.0, 0, -1))
+    e_qs = one(g.affine_select(T.qs[:, :], T.onesb[:, 0:8], [[-16, 8]], A.is_equal, 0.0, 0, 1))
+    e_lh = ev()
+    inc(e_lh, g.affine_select(T.lh[:, :], T.onesb[0:64, :], [[-1, 128]], A.is_equal, 0.0, 0, 2))
+    inc(e_lh, g.affine_select(T.ll[:, :], T.onesb[0:64, :], [[-1, 128]], A.is_equal, 0.0, 1, 2))
+    e_xj = one(g.iota(T.xj[:, :], [[1, 32]], 513, 32, allow_small_or_imprecise_dtypes=True))
+
+    w("V", e_lim)
+    e_lf = one(V.tensor_copy(T.lf[:, :], T.lm[:, :]))
+    w("P", e_lf, e_onesf)
+    e_lp = one(mm(T.p0[:, 0:2], T.onesf[0:1, :], T.lf[:, :]))
+    w("V", e_lp, e_a0)
+    e_f1 = one(V.tensor_scalar(T.f1[:, :], T.a0[:, :], T.p0[:, 0:1], None, A.is_ge))
+    e_f2 = one(V.tensor_scalar(T.f2[:, :], T.a0[:, :], T.p0[:, 1:2], None, A.is_gt))
+    w("P", e_w, e_f1)
+    mm(T.p7[:, 0:16], T.f1[:, :], T.wp[:, :], True, False)
+    w("P", e_f2)
+    e_pk = one(mm(T.p7[:, 0:16], T.f2[:, :], T.wn[:, :], False, True))
+    w("V", e_pk)
+    slot1 = T.pall[:, 16 * me:16 * me + 16]
+    e_pall = one(V.tensor_copy(slot1, T.p7[:, 0:16]))
+
+    w("g", e_pall)
+    m1 = send(x1, T.sem.x1, T.sem.l1, lambda r: slot1, slot1)
+
+    w("Y", e_slot)
+    e_at = ev()
+    for k in range(4):
+        for s in range(2):
+            p = 32 * k + 16 * s
+            inc(e_at, Y.dma_start(T.at2[p:p + 16, 1:HALF + 1], T["at"][:, HALF * s:HALF * s + HALF]), 16)
+        if k == 0:
+            Y.wait_ge(T.sem.l1, m1)
+
+    w("V", e_fk)
+    e_wi = one(V.tensor_scalar(T.wi[:, :], T.fks[:, :], 2047, None, A.bitwise_and))
+    e_bi = one(V.tensor_scalar(T.bi[:, :], T.fks[:, :], 11, None, A.arith_shift_right))
+    w("V", e_wi)
+    e_w16 = ev()
+    for h in range(2):
+        inc(e_w16, V.tensor_copy(T.w16[:, 128 * h:128 * h + 128], T.wi[:, h::2]))
+    w("V", e_bi)
+    e_bb = ev()
+    for h in range(2):
+        inc(e_bb, V.tensor_copy(T.bb[:, 128 * h:128 * h + 128], T.bi[:, h::2]))
+    w("S", e_bb)
+    e_rb = one(S.activation(T.rb[:, :], T.bb[:, :], Fn.Exp, scale=-math.log(2.0)))
+    w("P", e_rb, e_id)
+    e_rp = ev()
+    for h in range(2):
+        inc(e_rp, mm(T.p1[:, 128 * h:128 * h + 128], T.rb[:, 128 * h:128 * h + 128], T.idb[:, :]))
+    w("S", e_rp)
+    e_rt = one(S.activation(T.rt[:, :], T.p1[:, 0:256], Fn.Copy, scale=128.0))
+    w("V", e_vr)
+    e_vh = one(V.tensor_scalar(T.vh[:, :], T.vr[:, :], 7, None, A.arith_shift_right))
+    e_vl = one(V.tensor_scalar(T.vl[:, :], T.vr[:, :], 127, None, A.bitwise_and))
+    e_hl = ev()
+    w("V", e_vh)
+    for h in range(2):
+        inc(e_hl, V.tensor_copy(T.hb[:, 256 * h:256 * h + 256], T.vh[:, h::2]))
+    w("V", e_vl)
+    for h in range(2):
+        inc(e_hl, V.tensor_scalar(T.lb[:, 256 * h:256 * h + 256], T.vl[:, h::2], 1.0, None, A.add))
+    w("P", e_hl, e_lh)
+    mm(T.p6[:, :], T.lh[:, :], T.hb[:, :], True, False)
+    e_vp = one(mm(T.p6[:, :], T.ll[:, :], T.lb[:, :], False, True))
+    w("S", e_vp)
+    e_vb = one(S.activation(T.vb[:, :], T.p6[:, :], Fn.Copy))
+    e_win0 = one(V.memset(T.win[:, 0:512], 0.0))
+    e_selh = one(V.tensor_scalar(T.selh[:, :], T.m16[:, 0::2], 128.0, None, A.mult))
+    w("V", e_xj)
+    e_xj1 = one(V.tensor_scalar(T.xj1[:, :], T.xj[:, :], -1.0, None, A.add))
+    e_mn0 = one(V.memset(T.mn[:, :], 0))
+    e_sel20 = one(V.memset(T.sel2[:, :], 0.0))
+    w("Y", e_mn0)
+    e_mn = one(Y.dma_start(T.mn[0::16, :], T["me"][0:1, :]), 16)
+    w("V", e_selh)
+    e_sel = one(V.tensor_tensor(T.sel[:, :], T.selh[:, :], T.m16[:, 1::2], A.add))
+    w("g", e_onesf)
+    e_ax = ev()
+    inc(e_ax, g.affine_select(T.ax0[:, :], T.onesf[:, :], [[-32, 4], [0, 2], [-1, 16]], A.is_equal, 0.0, 0, 1))
+    inc(e_ax, g.affine_select(T.ax1[:, :], T.onesf[:, :], [[-32, 4], [0, 2], [-1, 16]], A.is_equal, 0.0, -16, 1))
+    e_ml = one(g.iota(T.ml[:, :], [[1, 32]], 0, 32))
+    w("g", e_sel20)
+    e_s2a = one(g.affine_select(T.sel2[:, :], T.sel2[:, :], [[-32, 4], [-1, 16]], A.not_equal, 1.0, 0, 1))
+    w("g", e_s2a)
+    e_sel2 = one(g.affine_select(T.sel2[:, :], T.sel2[:, :], [[-32, 4], [-1, 16]], A.not_equal, 1.0, -16, 1))
+    e_prm = one(g.affine_select(T.prm[:, :], T.onesf[:, :], [[-16, 2], [-1, 16], [-32, 4]], A.is_equal, 0.0, 0, 1))
+
+    P.wait_ge(T.sem.x1, n1)
+    w("P", e_pall)
+    e_t1 = one(mm(T.p7[:, 128:256], T.pall[:, :], T.idb[:, :]))
+    w("V", e_t1)
+    e_o1 = one(V.tensor_copy(T.o1[:, :], T.p7[:, 128:256]))
+    w("P", e_o1, e_sm)
+    e_w8 = ev()
+    for j in range(4):
+        bank = T["p%d" % (2 + j)]
+        e = ev()
+        for m in range(4):
+            k = 4 * j + m
+            inc(e, mm(bank[:, 128 * m:128 * m + 128], T.sm[:, 128 * k:128 * k + 128], T.o1[:, :]))
+        qn = "VS"[j % 2]
+        w(qn, e)
+        inc(e_w8, copy(qn, T.win8[:, 512 * j:512 * j + 512], bank[:, :]))
+    w("V", e_w8, e_w16)
+    w("S", e_w8, e_w16)
+    e_g = [ev(), ev()]
+    for h in range(2):
+        for half in range(2):
+            k = 2 * h + half
+            src = T.win8[:, :].indirect(T.w16[:, 64 * k:64 * k + 64])
+            inc(e_g[h], copy("VS"[half], T.gw[:, 1024 * k:1024 * k + 1024], src))
+
+    w("P", e_qs, e_rt, e_vb)
+    e_sv = ev()
+    for h in range(2):
+        bank = (T.p1, T.p6)[h]
+        w("P", e_g[h])
+        e = ev()
+        for p in range(16):
+            inc(e, mm(bank[:, p:128:16], T.gw[:, 2048 * h + p:2048 * h + 2048:16], T.qs[:, :]))
+        w("V", e, e_rt)
+        u, v, t, s = T["u%d" % h], T["v%d" % h], T["t%d" % h], T["s%d" % h]
+        e = one(V.tensor_tensor(u[:, :], bank[:, 0:128], T.rt[:, 128 * h:128 * h + 128], A.mult))
+        w("V", e)
+        e = one(V.tensor_scalar(v[:, :], u[:, :], 7, 1, A.logical_shift_right, A.bitwise_and))
+        w("V", e)
+        e = one(V.tensor_tensor(t[:, :], v[:, 0:64], v[:, 64:128], A.min))
+        w("V", e)
+        e = one(V.tensor_tensor(s[:, :], t[:, 0:32], t[:, 32:64], A.min))
+        w("V", e)
+        inc(e_sv, V.tensor_tensor(T.sv[:, 16 * h:16 * h + 16], s[:, 0:16], s[:, 16:32], A.min))
+
+    w("V", e_sv, e_zb)
+    e_cum = one(V.tensor_tensor_scan(T.cum[:, :], T.sv[:, :], T.zb[:, :], 0.0, A.add, A.add))
+    w("P", e_cum, e_tri)
+    e_base = one(mm(T.p0[:, 16:17], T.tri[:, :], T.cum[:, 31:32]))
+    e_e1 = one(V.tensor_tensor(T.e1[:, :], T.sv[:, :], T.xj[:, :], A.mult))
+    w("V", e_cum, e_xj1)
+    e_e2 = one(V.tensor_tensor(T.e2[:, :], T.cum[:, :], T.xj1[:, :], A.add))
+    w("V", e_e1, e_e2)
+    e_e3 = one(V.tensor_tensor(T.e3[:, :], T.e2[:, :], T.e1[:, :], A.subtract))
+    w("V", e_base, e_e3)
+    e_off = one(V.tensor_scalar(T.off[:, :], T.e3[:, :], T.p0[:, 16:17], None, A.add))
+    w("V", e_off, e_vb, e_win0)
+    e_sc = one(V.tensor_copy(T.win[:, 0:WIN].indirect(T.off[:, 0:32]), T.vb[:, :]))
+    w("P", e_sc, e_sel, e_sv)
+    e_ls = ev()
+    for b in range(4):
+        inc(e_ls, mm(T.p6[:, 128 + b:160:4], T.win[:, b:512:4], T.sel[:, :]))
+    w("V", e_ls)
+    e_z = one(V.tensor_copy(T.z[:, :], T.p6[:, 128:160]))
+    w("V", e_z)
+    slot2 = T.rx2[:, 4 * me:4 * me + 4]
+    e_own2 = one(V.tensor_copy(slot2, T.z[:, 4 * me:4 * me + 4]))
+
+    w("g", e_z)
+    m2 = send(x2, T.sem.x2, T.sem.l2, lambda r: T.z[:, 4 * r:4 * r + 4], slot2)
+
+    w("P", e_onesb)
+    e_cnt = one(mm(T.p7[0:64, 128:129], T.onesb[:, 0:64], T.cum[:, 31:32]))
+    e_sg = one(V.tensor_scalar(T.sg[:, :], T.gi[:, :], 1, None, A.bitwise_and))
+    w("V", e_ml)
+    e_ml2 = one(V.tensor_scalar(T.ml2[:, :], T.ml[:, :], 511, None, A.bitwise_and))
+    w("V", e_sg)
+    e_sgf = one(V.tensor_scalar(T.sgf[:, :], T.sg[:, :], float(HALF), None, A.mult))
+    w("V", e_ml2)
+    e_ml16 = one(V.tensor_copy(T.ml16[:, :], T.ml2[:, :]))
+    w("V", e_ml16, e_mn)
+    e_mv = one(V.tensor_copy(T.mv[:, :], T.mn[:, :].indirect(T.ml16[:, 0:32])))
+    e_mw0 = one(V.memset(T.mwin[:, 0:512], 0.0))
+    e_b70 = one(V.memset(T.b7[:, :], 0.0))
+    w("V", e_b70)
+    e_b7 = one(V.tensor_scalar(T.b7[:, 48:64], T.onesf[:, 0:16], T.m16f[:, 0:1], None, A.mult))
+
+    P.wait_ge(T.sem.x2, n2)
+    w("P", e_own2, e_ax)
+    e_tb = ev()
+    for xx in range(2):
+        inc(e_tb, mm(T.p0[:, 64 + xx:128:2], T["ax%d" % xx][:, :], T.rx2[:, :]))
+    w("V", e_tb, e_sgf)
+    e_off2 = one(V.tensor_scalar(T.off2[:, :], T.p0[:, 64:128], T.sgf[:, 0:1], float(HALF + 1), A.subtract, A.min))
+    w("V", e_off2, e_at)
+    w("S", e_off2, e_at)
+    e_ga = []
+    for k, (ch, rs) in enumerate(order):
+        r0 = rs[0]
+        src = T.at2[:, 0:HALF + 8].indirect(T.off2[:, 8 * r0:8 * r0 + 16])
+        e_ga.append(one(copy("VS"[k % 2], T.ga[:, 128 * r0:128 * r0 + 256], src)))
+    w("P", e_sel2)
+    e_zs = []
+    slot3 = T.rx3[:, 64 * me:64 * me + 64]
+    e_own3 = ev()
+    for k, (ch, rs) in enumerate(order):
+        bank = T["p%d" % (2 + k)]
+        w("P", e_ga[k])
+        e = ev()
+        for j, r in enumerate(rs):
+            inc(e, mm(bank[:, 64 * j:64 * j + 64], T.ga[:, 128 * r:128 * r + 128], T.sel2[:, :]))
+        qn = "VS"[k % 2]
+        w(qn, e)
+        e_zs.append(ev())
+        for j, r in enumerate(rs):
+            if r == me:
+                inc(e_own3, copy(qn, slot3, bank[:, 64 * j:64 * j + 64]))
+            else:
+                inc(e_zs[k], copy(qn, T.zs[:, 64 * r:64 * r + 64], bank[:, 64 * j:64 * j + 64]))
+
+    m3 = 0
+    for k, call in enumerate(x3):
+        w("g", e_zs[k])
+        m3 += send([call], T.sem.x3, T.sem.l3, lambda r: T.zs[:, 64 * r:64 * r + 64], slot3)
+
+    w("V", e_mv, e_mw0, e_off)
+    e_ms = one(V.tensor_copy(T.mwin[:, 0:WIN].indirect(T.off[:, 0:32]), T.mv[:, :]))
+    w("P", e_ms, e_b7, e_cnt)
+    for k in range(4):
+        mm(T.p7[0:64, 0:128], T.b7[:, 48 - 16 * k:112 - 16 * k], T.mwin[:, 128 * k:128 * k + 128], k == 0, False)
+
+    V.wait_ge(T.sem.x3, n3)
+    w("V", e_own3)
+    e = one(V.tensor_tensor(T.q1[:, :], T.rx3[:, 0:256], T.rx3[:, 256:512], A.add))
+    w("V", e)
+    e = one(V.tensor_tensor(T.q2[:, :], T.q1[:, 0:128], T.q1[:, 128:256], A.add))
+    w("V", e)
+    e = one(V.tensor_tensor(T.q3[:, :], T.q2[:, 0:64], T.q2[:, 64:128], A.add))
+    w("P", e, e_prm)
+    e_fin = one(mm(T.p7[0:64, 0:128], T.q3[:, :], T.prm[:, :], False, True))
+    w("V", e_fin)
+    e_yo = one(V.tensor_copy(T.yo[:, :], T.p7[0:64, 0:129]))
+    e_y = ev()
+    for k in range(4):
+        qn = "YS"[k % 2]
+        n = 129 if k == 3 else 128
+        w(qn, e_yo)
+        inc(e_y, names[qn].dma_start(T.y[:, 128 * k:128 * k + n], T.yo[16 * k:16 * k + 16, 0:n]), 16)
+    g.wait_ge(T.sem.l1, m1)
+    g.wait_ge(T.sem.l2, m2)
+    g.wait_ge(T.sem.l3, m3)
+    w("g", e_y)
+    for e in range(len(evs)):
+        if e not in waited:
+            w("g", e)

@@ -7,27 +7,22 @@ WIN = 5120
 HALF = 8192
 SCRATCH = {}
 for _t, _list in (
-        (BF, "f1 128,f2 128,pall 128,o1 128,onesb 128,zb 32,m16 16,gp 1,wp 16,wn 16,bd 128,sm 2048,idb 128,tri 128,qs 8,"
-             "bb 256,rb 256,vb 512,win8 2048,gw 4096,t0 64,t1 64,s0 32,s1 32,sv 32,cum 32,win 5120,sel 8,selh 8"),
+        (BF, "f1 128,f2 128,pall 128,o1 128,onesb 128,negb 64,m16 16,gp 1,wp 16,bd 128,sm 2048,idb 128,tri 128,qs 8,"
+             "bb 256,rb 256,vb 512,win8 2048,gw 4096,t0 64,t1 64,s0 32,s1 32,ns 32,cum 32,win 5120,sel 8,selh 8,"
+             "lh00 128,lh01 128,lh10 128,lh11 128,hl0 256,hl1 256"),
         (I32, "a0 128,im 16,im2 16,gi 1,ib 128,ib2 128,fks 256,wi 256,bi 256,u0 128,u1 128,v0 128,v1 128,sg 1,mn 512,"
-              "ml 32,ml2 32,at2 8200"),
-        (F32, "onesf 128,m16f 16,gf 1,gpf 1,xj 32,xj1 32,rt 256,e1 32,e2 32,e3 32,z 32,rx2 32,ax0 128,ax1 128,sgf 1,"
-              "ga 1024,sel2 64,zs 512,rx3 512,q1 256,q2 128,q3 64,prm 128,mv 512,mwin 5120,b7 112"),
+              "ml 32,ml2 32,at2 8200,vr 256,vh 256,vl 256"),
+        (F32, "onesf 128,m16f 16,gf 1,gpf 1,xj 32,rt 256,e1 32,e2 32,z 32,rx2 32,ax0 128,ax1 128,sgf 1,"
+              "ga 1024,sel2 64,zs 512,rx3 512,q1 128,q2 64,q3 128,q4 64,prm 128,mv 512,mwin 5120,b7 112"),
         (U16, "w16 256,off 32,off2 64,ml16 32")):
     for _x in _list.split(","):
         SCRATCH[_x.split()[0]] = ("sbuf", [128, int(_x.split()[1])], _t)
 SCRATCH["lm"] = ("sbuf", [1, 2], I32)
 SCRATCH["lf"] = ("sbuf", [1, 2], F32)
 SCRATCH["yo"] = ("sbuf", [64, 129], F32)
-for _k in ("lh", "ll"):
-    SCRATCH[_k] = ("sbuf", [64, 128], BF)
-for _k in ("vr", "vh", "vl"):
-    SCRATCH[_k] = ("sbuf", [64, 512], I32)
-for _k in ("hb", "lb"):
-    SCRATCH[_k] = ("sbuf", [64, 512], BF)
 for _k in range(8):
     SCRATCH["p%d" % _k] = ("psum", [128, 512], F32)
-SEMAPHORES = ["x1", "x2", "x3", "l1", "l2", "l3"] + ["e%d" % k for k in range(130)]
+SEMAPHORES = ["x1", "x2", "x3a", "x3b", "l1", "l2", "l3"] + ["e%d" % k for k in range(130)]
 
 
 def distance_order(core, T, topo):
@@ -49,6 +44,11 @@ def distance_order(core, T, topo):
     return out
 
 
+def slot_of(rank, sender, T, topo):
+    flat = [r for ch, rs in distance_order(T.cores[rank], T, topo) for r in rs if r != rank] + [rank]
+    return flat.index(sender)
+
+
 def plans(core, T, topo):
     me = T.rank_of(core)
     order = distance_order(core, T, topo)
@@ -63,10 +63,10 @@ def plans(core, T, topo):
     return order, x1, x2, x3
 
 
-def arriving(core, T, topo, which):
+def arriving(core, T, topo, which, slots=range(8)):
     me, n = T.rank_of(core), 0
     for c in T.cores:
-        if c != core:
+        if c != core and slot_of(me, T.rank_of(c), T, topo) in slots:
             for call in plans(c, T, topo)[which]:
                 for dests, eng in call:
                     if me in dests:
@@ -110,7 +110,8 @@ def rank_program(g, core, T, topo):
         return V.tensor_copy(out, in_) if qn == "V" else S.activation(out, in_, Fn.Copy)
 
     order, x1, x2, x3 = plans(core, T, topo)
-    n1, n2, n3 = [arriving(core, T, topo, k) for k in (1, 2, 3)]
+    n1, n2 = arriving(core, T, topo, 1), arriving(core, T, topo, 2)
+    n3a, n3b = arriving(core, T, topo, 3, range(4)), arriving(core, T, topo, 3, range(4, 8))
 
     def send(calls, rsem, lsem, src, dst):
         n = 0
@@ -121,24 +122,22 @@ def rank_program(g, core, T, topo):
                 for r in dests:
                     rid, pid, se = topo.addr(T.cores[r])
                     ids.append(DstId(rid=rid, pnc=pid))
-                tr.append(RemoteDMATransfer(dst_ids=ids, dma_engine_mask=sum(1 << e for e in eng), remote_sem=rsem,
-                                            srcs=[src(dests[0])], dsts=[dst] * len(dests)))
+                tr.append(RemoteDMATransfer(dst_ids=ids, dma_engine_mask=sum(1 << e for e in eng),
+                                            remote_sem=rsem(dests[0]), srcs=[src(dests[0])],
+                                            dsts=[dst(dests[0])] * len(dests)))
                 n += len(eng)
             g.remote_dma_fused(tr, local_sem=lsem)
         return n
 
     e_lim = one(S.dma_start(T.lm[:, :], T.lim[:, :]), 16)
     e_a0 = one(Y.dma_start(T.a0[:, :], T["at"][0:1, :]), 16)
-    e_fk = one(S.dma_start(T.fks[:, :], T.fk[:, :]), 16)
+    e_fk = one(Y.dma_start(T.fks[:, :], T.fk[:, :]), 16)
     e_vr = ev()
     for k in range(8):
-        inc(e_vr, Y.dma_start(T.vr[8 * k:8 * k + 8, :], T.fk[:, 32 * k:32 * k + 32]), 16)
+        inc(e_vr, Y.dma_start(T.vr[16 * k:16 * k + 16, :], T.fk[:, 32 * k:32 * k + 32]), 16)
 
     e_im = one(g.iota(T.im[:, :], [[-1, 16]], 0, 1))
     e_onesb = one(V.memset(T.onesb[:, :], 1.0))
-    e_slot = ev()
-    inc(e_slot, V.memset(T.at2[:, 0:1], 0))
-    inc(e_slot, V.memset(T.at2[:, HALF + 1:HALF + 8], 0))
     e_onesf = one(V.memset(T.onesf[:, :], 1.0))
     e_ib = one(g.iota(T.ib[:, :], [[-16, 8], [0, 16]], 0, 1))
     w("V", e_im)
@@ -152,68 +151,69 @@ def rank_program(g, core, T, topo):
     e_gp = one(S.activation(T.gp[:, :], T.gf[:, :], Fn.Exp, scale=math.log(2.0)))
     w("V", e_ib)
     e_ib2 = one(V.tensor_scalar(T.ib2[:, :], T.ib[:, :], 4, None, A.arith_shift_right))
-    w("V", e_ib2)
-    e_bd = one(V.tensor_scalar(T.bd[:, :], T.ib2[:, :], 0.0, None, A.is_equal))
     w("V", e_m16)
     e_m16f = one(V.tensor_copy(T.m16f[:, :], T.m16[:, :]))
-    e_zb = one(V.memset(T.zb[:, :], 0.0))
+    w("V", e_ib2)
+    e_bd = one(V.tensor_scalar(T.bd[:, :], T.ib2[:, :], 0.0, None, A.is_equal))
+    e_slot = ev()
+    inc(e_slot, V.memset(T.at2[:, 0:1], 0))
+    inc(e_slot, V.memset(T.at2[:, HALF + 1:HALF + 8], 0))
+    e_negb = one(V.memset(T.negb[:, :], -1.0))
     w("V", e_bd, e_m16f)
+    w("S", e_bd, e_m16f)
     e_sm = ev()
     for m in range(16):
-        inc(e_sm, V.tensor_scalar(T.sm[:, 128 * m:128 * m + 128], T.bd[:, :], T.m16f[:, m:m + 1], None, A.mult))
-    w("V", e_gp)
-    e_gpf = one(V.tensor_copy(T.gpf[:, :], T.gp[:, :]))
-    w("V", e_gpf)
-    e_w = ev()
-    inc(e_w, V.tensor_scalar(T.wp[:, :], T.m16[:, :], T.gpf[:, 0:1], None, A.mult))
-    inc(e_w, V.tensor_scalar(T.wn[:, :], T.m16[:, :], T.gpf[:, 0:1], -1.0, A.mult, A.mult))
+        out, col = T.sm[:, 128 * m:128 * m + 128], T.m16f[:, m:m + 1]
+        if m % 2 == 0:
+            inc(e_sm, V.tensor_scalar(out, T.bd[:, :], col, None, A.mult))
+        else:
+            inc(e_sm, S.activation(out, T.bd[:, :], Fn.Copy, scale=col))
     w("g", e_onesb)
     e_id = one(g.affine_select(T.idb[:, :], T.onesb[:, :], [[-1, 128]], A.is_equal, 0.0, 0, 1))
     e_tri = one(g.affine_select(T.tri[:, :], T.onesb[:, :], [[1, 128]], A.is_gt, 0.0, 0, -1))
     e_qs = one(g.affine_select(T.qs[:, :], T.onesb[:, 0:8], [[-16, 8]], A.is_equal, 0.0, 0, 1))
-    e_lh = ev()
-    inc(e_lh, g.affine_select(T.lh[:, :], T.onesb[0:64, :], [[-1, 128]], A.is_equal, 0.0, 0, 2))
-    inc(e_lh, g.affine_select(T.ll[:, :], T.onesb[0:64, :], [[-1, 128]], A.is_equal, 0.0, 1, 2))
-    e_xj = one(g.iota(T.xj[:, :], [[1, 32]], 513, 32, allow_small_or_imprecise_dtypes=True))
 
     w("V", e_lim)
     e_lf = one(V.tensor_copy(T.lf[:, :], T.lm[:, :]))
     w("P", e_lf, e_onesf)
     e_lp = one(mm(T.p0[:, 0:2], T.onesf[0:1, :], T.lf[:, :]))
+    w("V", e_gp)
+    e_gpf = one(V.tensor_copy(T.gpf[:, :], T.gp[:, :]))
+    w("V", e_gpf)
+    e_w = one(V.tensor_scalar(T.wp[:, :], T.m16[:, :], T.gpf[:, 0:1], None, A.mult))
     w("V", e_lp, e_a0)
-    e_f1 = one(V.tensor_scalar(T.f1[:, :], T.a0[:, :], T.p0[:, 0:1], None, A.is_ge))
+    e_f1 = one(V.tensor_scalar(T.f1[:, :], T.a0[:, :], T.p0[:, 0:1], None, A.is_lt))
     e_f2 = one(V.tensor_scalar(T.f2[:, :], T.a0[:, :], T.p0[:, 1:2], None, A.is_gt))
     w("P", e_w, e_f1)
     mm(T.p7[:, 0:16], T.f1[:, :], T.wp[:, :], True, False)
     w("P", e_f2)
-    e_pk = one(mm(T.p7[:, 0:16], T.f2[:, :], T.wn[:, :], False, True))
+    e_pk = one(mm(T.p7[:, 0:16], T.f2[:, :], T.wp[:, :], False, True))
     w("V", e_pk)
     slot1 = T.pall[:, 16 * me:16 * me + 16]
     e_pall = one(V.tensor_copy(slot1, T.p7[:, 0:16]))
 
     w("g", e_pall)
-    m1 = send(x1, T.sem.x1, T.sem.l1, lambda r: slot1, slot1)
+    m1 = send(x1, lambda r: T.sem.x1, T.sem.l1, lambda r: slot1, lambda r: slot1)
 
     w("Y", e_slot)
+    Y.wait_ge(T.sem.l1, m1)
     e_at = ev()
     for k in range(4):
         for s in range(2):
             p = 32 * k + 16 * s
             inc(e_at, Y.dma_start(T.at2[p:p + 16, 1:HALF + 1], T["at"][:, HALF * s:HALF * s + HALF]), 16)
-        if k == 0:
-            Y.wait_ge(T.sem.l1, m1)
 
     w("V", e_fk)
-    e_wi = one(V.tensor_scalar(T.wi[:, :], T.fks[:, :], 2047, None, A.bitwise_and))
     e_bi = one(V.tensor_scalar(T.bi[:, :], T.fks[:, :], 11, None, A.arith_shift_right))
-    w("V", e_wi)
-    e_w16 = ev()
-    for h in range(2):
-        inc(e_w16, V.tensor_copy(T.w16[:, 128 * h:128 * h + 128], T.wi[:, h::2]))
+    e_wi = one(V.tensor_scalar(T.wi[:, :], T.fks[:, :], 2047, None, A.bitwise_and))
     w("V", e_bi)
     e_bb = ev()
     for h in range(2):
         inc(e_bb, V.tensor_copy(T.bb[:, 128 * h:128 * h + 128], T.bi[:, h::2]))
+    w("V", e_wi)
+    e_w16 = ev()
+    for h in range(2):
+        inc(e_w16, V.tensor_copy(T.w16[:, 128 * h:128 * h + 128], T.wi[:, h::2]))
     w("S", e_bb)
     e_rb = one(S.activation(T.rb[:, :], T.bb[:, :], Fn.Exp, scale=-math.log(2.0)))
     w("P", e_rb, e_id)
@@ -228,35 +228,35 @@ def rank_program(g, core, T, topo):
     e_hl = ev()
     w("V", e_vh)
     for h in range(2):
-        inc(e_hl, V.tensor_copy(T.hb[:, 256 * h:256 * h + 256], T.vh[:, h::2]))
+        inc(e_hl, V.tensor_copy(T.hl0[:, 128 * h:128 * h + 128], T.vh[:, h::2]))
     w("V", e_vl)
     for h in range(2):
-        inc(e_hl, V.tensor_scalar(T.lb[:, 256 * h:256 * h + 256], T.vl[:, h::2], 1.0, None, A.add))
-    w("P", e_hl, e_lh)
-    mm(T.p6[:, :], T.lh[:, :], T.hb[:, :], True, False)
-    e_vp = one(mm(T.p6[:, :], T.ll[:, :], T.lb[:, :], False, True))
-    w("S", e_vp)
-    e_vb = one(S.activation(T.vb[:, :], T.p6[:, :], Fn.Copy))
-    e_win0 = one(V.memset(T.win[:, 0:512], 0.0))
+        inc(e_hl, V.tensor_scalar(T.hl1[:, 128 * h:128 * h + 128], T.vl[:, h::2], 1.0, None, A.add))
     e_selh = one(V.tensor_scalar(T.selh[:, :], T.m16[:, 0::2], 128.0, None, A.mult))
-    w("V", e_xj)
-    e_xj1 = one(V.tensor_scalar(T.xj1[:, :], T.xj[:, :], -1.0, None, A.add))
-    e_mn0 = one(V.memset(T.mn[:, :], 0))
     e_sel20 = one(V.memset(T.sel2[:, :], 0.0))
-    w("Y", e_mn0)
-    e_mn = one(Y.dma_start(T.mn[0::16, :], T["me"][0:1, :]), 16)
     w("V", e_selh)
     e_sel = one(V.tensor_tensor(T.sel[:, :], T.selh[:, :], T.m16[:, 1::2], A.add))
+    e_lh = ev()
+    for x in range(2):
+        for hl in range(2):
+            inc(e_lh, g.affine_select(T["lh%d%d" % (x, hl)][:, :], T.onesb[:, :], [[-2, 64], [1000, 2]], A.is_equal, 0.0,
+                                      -x - 1000 * hl, 1))
+    e_xj = one(g.iota(T.xj[:, :], [[1, 32]], 513, 32, allow_small_or_imprecise_dtypes=True))
+    e_win0 = one(g.iota(T.win[:, 0:512], [[0, 512]], 0, 0, allow_small_or_imprecise_dtypes=True))
+    e_mn0 = one(g.iota(T.mn[:, :], [[0, 512]], 0, 0))
+    w("Y", e_mn0)
+    e_mn = one(Y.dma_start(T.mn[0::16, :], T["me"][0:1, :]), 16)
     w("g", e_onesf)
     e_ax = ev()
     inc(e_ax, g.affine_select(T.ax0[:, :], T.onesf[:, :], [[-32, 4], [0, 2], [-1, 16]], A.is_equal, 0.0, 0, 1))
     inc(e_ax, g.affine_select(T.ax1[:, :], T.onesf[:, :], [[-32, 4], [0, 2], [-1, 16]], A.is_equal, 0.0, -16, 1))
-    e_ml = one(g.iota(T.ml[:, :], [[1, 32]], 0, 32))
     w("g", e_sel20)
     e_s2a = one(g.affine_select(T.sel2[:, :], T.sel2[:, :], [[-32, 4], [-1, 16]], A.not_equal, 1.0, 0, 1))
+    e_ml = one(g.iota(T.ml[:, :], [[1, 32]], 0, 32))
     w("g", e_s2a)
     e_sel2 = one(g.affine_select(T.sel2[:, :], T.sel2[:, :], [[-32, 4], [-1, 16]], A.not_equal, 1.0, -16, 1))
     e_prm = one(g.affine_select(T.prm[:, :], T.onesf[:, :], [[-16, 2], [-1, 16], [-32, 4]], A.is_equal, 0.0, 0, 1))
+    e_mw0 = one(g.iota(T.mwin[:, 0:512], [[0, 512]], 0, 0, allow_small_or_imprecise_dtypes=True))
 
     P.wait_ge(T.sem.x1, n1)
     w("P", e_pall)
@@ -265,15 +265,16 @@ def rank_program(g, core, T, topo):
     e_o1 = one(V.tensor_copy(T.o1[:, :], T.p7[:, 128:256]))
     w("P", e_o1, e_sm)
     e_w8 = ev()
-    for j in range(4):
+    k = 0
+    for j, n in enumerate((4, 4, 4, 2, 2)):
         bank = T["p%d" % (2 + j)]
         e = ev()
-        for m in range(4):
-            k = 4 * j + m
-            inc(e, mm(bank[:, 128 * m:128 * m + 128], T.sm[:, 128 * k:128 * k + 128], T.o1[:, :]))
-        qn = "VS"[j % 2]
+        for m in range(n):
+            inc(e, mm(bank[:, 128 * m:128 * m + 128], T.sm[:, 128 * (k + m):128 * (k + m) + 128], T.o1[:, :]))
+        qn = "VSVSV"[j]
         w(qn, e)
-        inc(e_w8, copy(qn, T.win8[:, 512 * j:512 * j + 512], bank[:, :]))
+        inc(e_w8, copy(qn, T.win8[:, 128 * k:128 * (k + n)], bank[:, 0:128 * n]))
+        k += n
     w("V", e_w8, e_w16)
     w("S", e_w8, e_w16)
     e_g = [ev(), ev()]
@@ -282,9 +283,18 @@ def rank_program(g, core, T, topo):
             k = 2 * h + half
             src = T.win8[:, :].indirect(T.w16[:, 64 * k:64 * k + 64])
             inc(e_g[h], copy("VS"[half], T.gw[:, 1024 * k:1024 * k + 1024], src))
+    w("P", e_hl, e_lh, e_w8)
+    e_vp = ev()
+    for h in range(2):
+        for x in range(2):
+            out = T.p2[:, 256 * h + 128 * x:256 * h + 128 * x + 128]
+            mm(out, T["lh%d0" % x][:, :], T.hl0[:, 128 * h:128 * h + 128], True, False)
+            inc(e_vp, mm(out, T["lh%d1" % x][:, :], T.hl1[:, 128 * h:128 * h + 128], False, True))
+    w("S", e_vp)
+    e_vb = one(S.activation(T.vb[:, :], T.p2[:, :], Fn.Copy))
 
-    w("P", e_qs, e_rt, e_vb)
-    e_sv = ev()
+    w("P", e_qs, e_rt)
+    e_ns = ev()
     for h in range(2):
         bank = (T.p1, T.p6)[h]
         w("P", e_g[h])
@@ -297,26 +307,25 @@ def rank_program(g, core, T, topo):
         w("V", e)
         e = one(V.tensor_scalar(v[:, :], u[:, :], 7, 1, A.logical_shift_right, A.bitwise_and))
         w("V", e)
-        e = one(V.tensor_tensor(t[:, :], v[:, 0:64], v[:, 64:128], A.min))
+        e = one(V.tensor_tensor(t[:, :], v[:, 0:64], v[:, 64:128], A.max))
         w("V", e)
-        e = one(V.tensor_tensor(s[:, :], t[:, 0:32], t[:, 32:64], A.min))
+        e = one(V.tensor_tensor(s[:, :], t[:, 0:32], t[:, 32:64], A.max))
         w("V", e)
-        inc(e_sv, V.tensor_tensor(T.sv[:, 16 * h:16 * h + 16], s[:, 0:16], s[:, 16:32], A.min))
+        inc(e_ns, V.tensor_tensor(T.ns[:, 16 * h:16 * h + 16], s[:, 0:16], s[:, 16:32], A.max))
 
-    w("V", e_sv, e_zb)
-    e_cum = one(V.tensor_tensor_scan(T.cum[:, :], T.sv[:, :], T.zb[:, :], 0.0, A.add, A.add))
+    w("V", e_ns, e_onesb)
+    e_cum = one(V.tensor_tensor_scan(T.cum[:, :], T.ns[:, :], T.onesb[:, 0:32], 0.0, A.add, A.subtract))
     w("P", e_cum, e_tri)
     e_base = one(mm(T.p0[:, 16:17], T.tri[:, :], T.cum[:, 31:32]))
-    e_e1 = one(V.tensor_tensor(T.e1[:, :], T.sv[:, :], T.xj[:, :], A.mult))
-    w("V", e_cum, e_xj1)
-    e_e2 = one(V.tensor_tensor(T.e2[:, :], T.cum[:, :], T.xj1[:, :], A.add))
-    w("V", e_e1, e_e2)
-    e_e3 = one(V.tensor_tensor(T.e3[:, :], T.e2[:, :], T.e1[:, :], A.subtract))
-    w("V", e_base, e_e3)
-    e_off = one(V.tensor_scalar(T.off[:, :], T.e3[:, :], T.p0[:, 16:17], None, A.add))
+    w("V", e_xj)
+    e_e1 = one(V.tensor_tensor(T.e1[:, :], T.ns[:, :], T.xj[:, :], A.mult))
+    w("V", e_cum, e_e1)
+    e_e2 = one(V.tensor_tensor(T.e2[:, :], T.e1[:, :], T.cum[:, :], A.subtract))
+    w("V", e_base, e_e2)
+    e_off = one(V.tensor_scalar(T.off[:, :], T.e2[:, :], T.p0[:, 16:17], 1.0, A.subtract, A.subtract))
     w("V", e_off, e_vb, e_win0)
     e_sc = one(V.tensor_copy(T.win[:, 0:WIN].indirect(T.off[:, 0:32]), T.vb[:, :]))
-    w("P", e_sc, e_sel, e_sv)
+    w("P", e_sc, e_sel, e_ns)
     e_ls = ev()
     for b in range(4):
         inc(e_ls, mm(T.p6[:, 128 + b:160:4], T.win[:, b:512:4], T.sel[:, :]))
@@ -327,20 +336,19 @@ def rank_program(g, core, T, topo):
     e_own2 = one(V.tensor_copy(slot2, T.z[:, 4 * me:4 * me + 4]))
 
     w("g", e_z)
-    m2 = send(x2, T.sem.x2, T.sem.l2, lambda r: T.z[:, 4 * r:4 * r + 4], slot2)
+    m2 = send(x2, lambda r: T.sem.x2, T.sem.l2, lambda r: T.z[:, 4 * r:4 * r + 4], lambda r: slot2)
 
-    w("P", e_onesb)
-    e_cnt = one(mm(T.p7[0:64, 128:129], T.onesb[:, 0:64], T.cum[:, 31:32]))
-    e_sg = one(V.tensor_scalar(T.sg[:, :], T.gi[:, :], 1, None, A.bitwise_and))
+    w("P", e_negb)
+    e_cnt = one(mm(T.p7[0:64, 128:129], T.negb[:, :], T.cum[:, 31:32]))
     w("V", e_ml)
     e_ml2 = one(V.tensor_scalar(T.ml2[:, :], T.ml[:, :], 511, None, A.bitwise_and))
-    w("V", e_sg)
-    e_sgf = one(V.tensor_scalar(T.sgf[:, :], T.sg[:, :], float(HALF), None, A.mult))
+    e_sg = one(V.tensor_scalar(T.sg[:, :], T.gi[:, :], 1, None, A.bitwise_and))
     w("V", e_ml2)
     e_ml16 = one(V.tensor_copy(T.ml16[:, :], T.ml2[:, :]))
-    w("V", e_ml16, e_mn)
-    e_mv = one(V.tensor_copy(T.mv[:, :], T.mn[:, :].indirect(T.ml16[:, 0:32])))
-    e_mw0 = one(V.memset(T.mwin[:, 0:512], 0.0))
+    w("V", e_sg)
+    e_sgf = one(V.tensor_scalar(T.sgf[:, :], T.sg[:, :], float(HALF), None, A.mult))
+    w("S", e_ml16, e_mn)
+    e_mv = one(S.activation(T.mv[:, :], T.mn[:, :].indirect(T.ml16[:, 0:32]), Fn.Copy))
     e_b70 = one(V.memset(T.b7[:, :], 0.0))
     w("V", e_b70)
     e_b7 = one(V.tensor_scalar(T.b7[:, 48:64], T.onesf[:, 0:16], T.m16f[:, 0:1], None, A.mult))
@@ -359,9 +367,9 @@ def rank_program(g, core, T, topo):
         r0 = rs[0]
         src = T.at2[:, 0:HALF + 8].indirect(T.off2[:, 8 * r0:8 * r0 + 16])
         e_ga.append(one(copy("VS"[k % 2], T.ga[:, 128 * r0:128 * r0 + 256], src)))
-    w("P", e_sel2)
+    w("P", e_sel2, e_vb)
     e_zs = []
-    slot3 = T.rx3[:, 64 * me:64 * me + 64]
+    slot3 = T.rx3[:, 448:512]
     e_own3 = ev()
     for k, (ch, rs) in enumerate(order):
         bank = T["p%d" % (2 + k)]
@@ -378,10 +386,14 @@ def rank_program(g, core, T, topo):
             else:
                 inc(e_zs[k], copy(qn, T.zs[:, 64 * r:64 * r + 64], bank[:, 64 * j:64 * j + 64]))
 
+    def land3(r):
+        k = slot_of(r, me, T, topo)
+        return T.rx3[:, 64 * k:64 * k + 64]
     m3 = 0
     for k, call in enumerate(x3):
         w("g", e_zs[k])
-        m3 += send([call], T.sem.x3, T.sem.l3, lambda r: T.zs[:, 64 * r:64 * r + 64], slot3)
+        m3 += send([call], lambda r: T.sem.x3a if slot_of(r, me, T, topo) < 4 else T.sem.x3b, T.sem.l3,
+                   lambda r: T.zs[:, 64 * r:64 * r + 64], land3)
 
     w("V", e_mv, e_mw0, e_off)
     e_ms = one(V.tensor_copy(T.mwin[:, 0:WIN].indirect(T.off[:, 0:32]), T.mv[:, :]))
@@ -389,15 +401,19 @@ def rank_program(g, core, T, topo):
     for k in range(4):
         mm(T.p7[0:64, 0:128], T.b7[:, 48 - 16 * k:112 - 16 * k], T.mwin[:, 128 * k:128 * k + 128], k == 0, False)
 
-    V.wait_ge(T.sem.x3, n3)
-    w("V", e_own3)
-    e = one(V.tensor_tensor(T.q1[:, :], T.rx3[:, 0:256], T.rx3[:, 256:512], A.add))
+    V.wait_ge(T.sem.x3a, n3a)
+    e = one(V.tensor_tensor(T.q1[:, :], T.rx3[:, 0:128], T.rx3[:, 128:256], A.add))
     w("V", e)
-    e = one(V.tensor_tensor(T.q2[:, :], T.q1[:, 0:128], T.q1[:, 128:256], A.add))
-    w("V", e)
-    e = one(V.tensor_tensor(T.q3[:, :], T.q2[:, 0:64], T.q2[:, 64:128], A.add))
+    e = one(V.tensor_tensor(T.q2[:, :], T.q1[:, 0:64], T.q1[:, 64:128], A.add))
     w("P", e, e_prm)
-    e_fin = one(mm(T.p7[0:64, 0:128], T.q3[:, :], T.prm[:, :], False, True))
+    mm(T.p7[0:64, 0:128], T.q2[:, :], T.prm[:, :], False, False)
+    V.wait_ge(T.sem.x3b, n3b)
+    w("V", e_own3)
+    e = one(V.tensor_tensor(T.q3[:, :], T.rx3[:, 256:384], T.rx3[:, 384:512], A.add))
+    w("V", e)
+    e = one(V.tensor_tensor(T.q4[:, :], T.q3[:, 0:64], T.q3[:, 64:128], A.add))
+    w("P", e)
+    e_fin = one(mm(T.p7[0:64, 0:128], T.q4[:, :], T.prm[:, :], False, True))
     w("V", e_fin)
     e_yo = one(V.tensor_copy(T.yo[:, :], T.p7[0:64, 0:129]))
     e_y = ev()

@@ -4,25 +4,45 @@ from concourse.mybir import AluOpType as A, ActivationFunctionType as Fn
 
 F32, BF, I32, U16 = "float32", "bfloat16", "int32", "uint16"
 WIN = 5120
-HALF = 8192
+ROWS = 16384
+PARTS = (2816, 2304, 2304)
+OWN = ROWS - sum(PARTS)
 SCRATCH = {}
 for _t, _list in (
-        (BF, "f1 128,f2 128,pall 128,o1 128,onesb 128,negb 64,m16 16,gp 1,wp 16,bd 128,sm 2048,idb 128,tri 128,qs 8,"
-             "bb 256,rb 256,vb 512,win8 2048,gw 4096,t0 64,t1 64,s0 32,s1 32,ns 32,cum 32,win 5120,sel 8,selh 8,"
+        (BF, "f1 128,f2 128,pall 128,o1 128,onesb 128,negb 128,m16 16,gp 1,wp 16,bd 128,sm 2048,idb 128,tri 128,qs 8,"
+             "bb 256,rb 256,vb 512,win8 2048,gw 4096,tt 128,sc 128,msk 128,cum 32,win 5120,sel 8,selh 8,"
              "lh00 128,lh01 128,lh10 128,lh11 128,hl0 256,hl1 256"),
-        (I32, "a0 128,im 16,im2 16,gi 1,ib 128,ib2 128,fks 256,wi 256,bi 256,u0 128,u1 128,v0 128,v1 128,sg 1,mn 512,"
-              "ml 32,ml2 32,at2 8200,vr 256,vh 256,vl 256"),
-        (F32, "onesf 128,m16f 16,gf 1,gpf 1,xj 32,rt 256,e1 32,e2 32,z 32,rx2 32,ax0 128,ax1 128,sgf 1,"
-              "ga 1024,sel2 64,zs 512,rx3 512,q1 128,q2 64,q3 128,q4 64,prm 128,mv 512,mwin 5120,b7 112"),
-        (U16, "w16 256,off 32,off2 64,ml16 32")):
+        (I32, "a0 128,im 16,im2 16,gi 1,ib 128,ib2 128,fks 256,wi 256,bi 256,u0 128,u1 128,v0 128,v1 128,mn 512,"
+              "ml 32,ml2 32,at2 16392,vr 256,vh 256,vl 256,hw 2816"),
+        (F32, "onesf 128,m16f 16,gf 1,gpf 1,xj 32,rt 256,e1 32,e2 32,ga 512,rx3 512,q1 128,q2 64,q3 128,qm 64,"
+              "mv 512,mwin 5120,b7 240,yo 68"),
+        (U16, "w16 256,off 32,off2 32,offo 8,ml16 32,z16 32")):
     for _x in _list.split(","):
         SCRATCH[_x.split()[0]] = ("sbuf", [128, int(_x.split()[1])], _t)
+for _k in range(3):
+    SCRATCH["hd%d" % _k] = ("dram", [2, 128, PARTS[_k] // 16], I32)
+    SCRATCH["raw%d" % _k] = ("sbuf", [128, PARTS[_k] // 8], I32)
 SCRATCH["lm"] = ("sbuf", [1, 2], I32)
 SCRATCH["lf"] = ("sbuf", [1, 2], F32)
-SCRATCH["yo"] = ("sbuf", [64, 129], F32)
 for _k in range(8):
     SCRATCH["p%d" % _k] = ("psum", [128, 512], F32)
-SEMAPHORES = ["x1", "x2", "x3a", "x3b", "l1", "l2", "l3"] + ["e%d" % k for k in range(130)]
+SEMAPHORES = ["x1", "x2", "x3a", "x3b", "l0", "l1", "l2", "l3", "hr", "wn"] + ["e%d" % k for k in range(130)]
+
+
+def helpers(core, T, topo):
+    hs = [c for c in topo.cores_of(core) if c not in T.cores and topo.die(c) == topo.die(core)]
+    return hs[:len(PARTS)]
+
+
+def part_start(i, t=0):
+    return 1 + OWN + sum(PARTS[:i]) + t * PARTS[i] // 2
+
+
+def helper_engines(core, T, topo):
+    hs = helpers(core, T, topo)
+    e = topo.engines(core, hs[0])
+    h, q = len(e) // 2, len(e) // 4
+    return [[e[:h], e[h:]], [e[:q], e[q:2 * q]], [e[2 * q:3 * q], e[3 * q:]]]
 
 
 def distance_order(core, T, topo):
@@ -59,7 +79,8 @@ def plans(core, T, topo):
     x1 = [[(far, eo), (near, en[:2])]]
     x2 = [[([far[k]], eo[2 * k:2 * k + 2]) for k in range(4)] + [(near, en[:2])],
           [([far[4 + k]], eo[4 * k:4 * k + 4]) for k in range(2)]]
-    x3 = [[([far[2 * k]], eo[0:4]), ([far[2 * k + 1]], eo[4:8])] for k in range(3)] + [[(near, en[:4])]]
+    x3 = [[([far[k]], eo[2 * k:2 * k + 2]) for k in range(4)],
+          [([far[4 + k]], eo[4 * k:4 * k + 4]) for k in range(2)] + [(near, en[:4])]]
     return order, x1, x2, x3
 
 
@@ -74,9 +95,41 @@ def arriving(core, T, topo, which, slots=range(8)):
     return n
 
 
+def transfer(dest_cores, eng, rsem, src, dst, topo):
+    ids = []
+    for c in dest_cores:
+        rid, pid, se = topo.addr(c)
+        ids.append(DstId(rid=rid, pnc=pid))
+    return RemoteDMATransfer(dst_ids=ids, dma_engine_mask=sum(1 << e for e in eng), remote_sem=rsem, srcs=[src],
+                             dsts=[dst] * len(ids))
+
+
+def helper_program(g, core, T, topo):
+    owners = [c for c in T.cores if core in helpers(c, T, topo)]
+    if not owners:
+        return
+    owner = owners[0]
+    i = helpers(owner, T, topo).index(core)
+    n = PARTS[i] // 2
+    for q in (g.sync, g.scalar):
+        q.wait_ge(T.sem.hr, sum(len(e) for e in helper_engines(owner, T, topo)[i]))
+    for t in range(2):
+        for k in range(8):
+            q = (g.sync, g.scalar)[k % 2]
+            q.dma_start(T.hw[16 * k:16 * k + 16, n * t:n * t + n], T["hd%d" % i][t]).then_inc(T.sem["e%d" % t], 16)
+    eng = topo.engines(core, owner)
+    for t in range(2):
+        g.wait_ge(T.sem["e%d" % t], 128)
+        c0 = part_start(i, t)
+        g.remote_dma_fused([transfer([owner], eng, T.sem.wn, T.hw[:, n * t:n * t + n], T.at2[:, c0:c0 + n], topo)],
+                           local_sem=T.sem.l0)
+    g.wait_ge(T.sem.l0, 2 * len(eng))
+
+
 def rank_program(g, core, T, topo):
     me = T.rank_of(core)
     if me is None:
+        helper_program(g, core, T, topo)
         return
     V, S, P, Y = g.vector, g.scalar, g.tensor, g.sync
     names = {"g": g, "V": V, "S": S, "P": P, "Y": Y}
@@ -112,29 +165,41 @@ def rank_program(g, core, T, topo):
     order, x1, x2, x3 = plans(core, T, topo)
     n1, n2 = arriving(core, T, topo, 1), arriving(core, T, topo, 2)
     n3a, n3b = arriving(core, T, topo, 3, range(4)), arriving(core, T, topo, 3, range(4, 8))
+    hs, heng = helpers(core, T, topo), helper_engines(core, T, topo)
+    nw = sum(2 * len(topo.engines(h, core)) for h in hs)
+    m0 = sum(len(e) for h in heng for e in h)
 
     def send(calls, rsem, lsem, src, dst):
         n = 0
         for call in calls:
-            tr = []
-            for dests, eng in call:
-                ids = []
-                for r in dests:
-                    rid, pid, se = topo.addr(T.cores[r])
-                    ids.append(DstId(rid=rid, pnc=pid))
-                tr.append(RemoteDMATransfer(dst_ids=ids, dma_engine_mask=sum(1 << e for e in eng),
-                                            remote_sem=rsem(dests[0]), srcs=[src(dests[0])],
-                                            dsts=[dst(dests[0])] * len(dests)))
-                n += len(eng)
-            g.remote_dma_fused(tr, local_sem=lsem)
+            g.remote_dma_fused([transfer([T.cores[r] for r in dests], eng, rsem(dests[0]), src(dests[0]), dst(dests[0]),
+                                         topo) for dests, eng in call], local_sem=lsem)
+            n += sum(len(eng) for dests, eng in call)
         return n
+
+    def raw(i, t):
+        n = PARTS[i] // 16
+        return T["raw%d" % i][:, n * t:n * t + n]
+
+    def send_raw(which):
+        g.remote_dma_fused([transfer([hs[i]], heng[i][t], T.sem.hr, raw(i, t), T["hd%d" % i][t], topo)
+                            for i in which for t in range(2)], local_sem=T.sem.l0)
+
+    def raw_load(q, i):
+        e = ev()
+        for t in range(2):
+            c0 = part_start(i, t) - 1
+            inc(e, q.dma_start(raw(i, t), T["at"][:, c0:c0 + PARTS[i] // 2]), 16)
+        return e
 
     e_lim = one(S.dma_start(T.lm[:, :], T.lim[:, :]), 16)
     e_a0 = one(Y.dma_start(T.a0[:, :], T["at"][0:1, :]), 16)
-    e_fk = one(Y.dma_start(T.fks[:, :], T.fk[:, :]), 16)
+    e_fk = one(S.dma_start(T.fks[:, :], T.fk[:, :]), 16)
+    e_raw = [raw_load(Y, 0)]
     e_vr = ev()
     for k in range(8):
         inc(e_vr, Y.dma_start(T.vr[16 * k:16 * k + 16, :], T.fk[:, 32 * k:32 * k + 32]), 16)
+    e_raw += [raw_load(Y, 1), raw_load(Y, 2)]
 
     e_im = one(g.iota(T.im[:, :], [[-1, 16]], 0, 1))
     e_onesb = one(V.memset(T.onesb[:, :], 1.0))
@@ -155,16 +220,12 @@ def rank_program(g, core, T, topo):
     e_m16f = one(V.tensor_copy(T.m16f[:, :], T.m16[:, :]))
     w("V", e_ib2)
     e_bd = one(V.tensor_scalar(T.bd[:, :], T.ib2[:, :], 0.0, None, A.is_equal))
-    e_slot = ev()
-    inc(e_slot, V.memset(T.at2[:, 0:1], 0))
-    inc(e_slot, V.memset(T.at2[:, HALF + 1:HALF + 8], 0))
-    e_negb = one(V.memset(T.negb[:, :], -1.0))
     w("V", e_bd, e_m16f)
     w("S", e_bd, e_m16f)
     e_sm = ev()
     for m in range(16):
         out, col = T.sm[:, 128 * m:128 * m + 128], T.m16f[:, m:m + 1]
-        if m % 2 == 0:
+        if m % 4 == 0:
             inc(e_sm, V.tensor_scalar(out, T.bd[:, :], col, None, A.mult))
         else:
             inc(e_sm, S.activation(out, T.bd[:, :], Fn.Copy, scale=col))
@@ -172,6 +233,10 @@ def rank_program(g, core, T, topo):
     e_id = one(g.affine_select(T.idb[:, :], T.onesb[:, :], [[-1, 128]], A.is_equal, 0.0, 0, 1))
     e_tri = one(g.affine_select(T.tri[:, :], T.onesb[:, :], [[1, 128]], A.is_gt, 0.0, 0, -1))
     e_qs = one(g.affine_select(T.qs[:, :], T.onesb[:, 0:8], [[-16, 8]], A.is_equal, 0.0, 0, 1))
+    e_ml = one(g.iota(T.ml[:, :], [[1, 32]], 0, 32))
+
+    w("g", e_raw[0])
+    send_raw([0])
 
     w("V", e_lim)
     e_lf = one(V.tensor_copy(T.lf[:, :], T.lm[:, :]))
@@ -191,17 +256,36 @@ def rank_program(g, core, T, topo):
     w("V", e_pk)
     slot1 = T.pall[:, 16 * me:16 * me + 16]
     e_pall = one(V.tensor_copy(slot1, T.p7[:, 0:16]))
+    e_slot = one(V.memset(T.at2[:, 0:1], 0))
 
     w("g", e_pall)
     m1 = send(x1, lambda r: T.sem.x1, T.sem.l1, lambda r: slot1, lambda r: slot1)
+    w("g", e_raw[1], e_raw[2])
+    send_raw([1, 2])
+
+    e_mn0 = one(g.iota(T.mn[:, :], [[0, 512]], 0, 0))
+    e_msk = one(g.affine_select(T.msk[:, :], T.onesb[:, :], [[0, 32], [1, 4]], A.not_equal, 0.0, 0, 0))
+    e_lh = ev()
+    for x in range(2):
+        for hl in range(2):
+            inc(e_lh, g.affine_select(T["lh%d%d" % (x, hl)][:, :], T.onesb[:, :], [[-2, 64], [1000, 2]], A.is_equal, 0.0,
+                                      -x - 1000 * hl, 1))
+    e_xj = one(g.iota(T.xj[:, :], [[1, 32]], 513, 32, allow_small_or_imprecise_dtypes=True))
+    e_win0 = one(g.iota(T.win[:, 0:512], [[0, 512]], 0, 0, allow_small_or_imprecise_dtypes=True))
+    e_mw0 = one(g.iota(T.mwin[:, 0:512], [[0, 512]], 0, 0, allow_small_or_imprecise_dtypes=True))
+    e_negb = one(g.iota(T.negb[:, :], [[0, 128]], -1, 0, allow_small_or_imprecise_dtypes=True))
+    e_b70 = one(g.iota(T.b7[:, :], [[0, 240]], 1, 0, allow_small_or_imprecise_dtypes=True))
+    w("g", e_b70)
+    e_b7 = one(g.affine_select(T.b7[:, :], T.b7[:, :], [[1, 15], [0, 16]], A.is_equal, 0.0, -7, 0))
 
     w("Y", e_slot)
     Y.wait_ge(T.sem.l1, m1)
     e_at = ev()
-    for k in range(4):
-        for s in range(2):
-            p = 32 * k + 16 * s
-            inc(e_at, Y.dma_start(T.at2[p:p + 16, 1:HALF + 1], T["at"][:, HALF * s:HALF * s + HALF]), 16)
+    for k in range(8):
+        inc(e_at, Y.dma_start(T.at2[16 * k:16 * k + 16, 1:OWN + 1], T["at"][:, 0:OWN]), 16)
+        if k == 3:
+            w("Y", e_mn0)
+            e_mn = one(Y.dma_start(T.mn[0::16, :], T["me"][0:1, :]), 16)
 
     w("V", e_fk)
     e_bi = one(V.tensor_scalar(T.bi[:, :], T.fks[:, :], 11, None, A.arith_shift_right))
@@ -219,44 +303,20 @@ def rank_program(g, core, T, topo):
     w("P", e_rb, e_id)
     e_rp = ev()
     for h in range(2):
-        inc(e_rp, mm(T.p1[:, 128 * h:128 * h + 128], T.rb[:, 128 * h:128 * h + 128], T.idb[:, :]))
+        for d in range(8):
+            inc(e_rp, mm(T.p1[:, 128 * h + d:128 * h + 128:8], T.rb[:, 128 * h:128 * h + 128],
+                         T.idb[:, 16 * d:16 * d + 16]))
     w("S", e_rp)
     e_rt = one(S.activation(T.rt[:, :], T.p1[:, 0:256], Fn.Copy, scale=128.0))
     w("V", e_vr)
     e_vh = one(V.tensor_scalar(T.vh[:, :], T.vr[:, :], 7, None, A.arith_shift_right))
-    e_vl = one(V.tensor_scalar(T.vl[:, :], T.vr[:, :], 127, None, A.bitwise_and))
+    e_selh = one(V.tensor_scalar(T.selh[:, :], T.m16[:, 0::2], 128.0, None, A.mult))
     e_hl = ev()
     w("V", e_vh)
     for h in range(2):
         inc(e_hl, V.tensor_copy(T.hl0[:, 128 * h:128 * h + 128], T.vh[:, h::2]))
-    w("V", e_vl)
-    for h in range(2):
-        inc(e_hl, V.tensor_scalar(T.hl1[:, 128 * h:128 * h + 128], T.vl[:, h::2], 1.0, None, A.add))
-    e_selh = one(V.tensor_scalar(T.selh[:, :], T.m16[:, 0::2], 128.0, None, A.mult))
-    e_sel20 = one(V.memset(T.sel2[:, :], 0.0))
     w("V", e_selh)
     e_sel = one(V.tensor_tensor(T.sel[:, :], T.selh[:, :], T.m16[:, 1::2], A.add))
-    e_lh = ev()
-    for x in range(2):
-        for hl in range(2):
-            inc(e_lh, g.affine_select(T["lh%d%d" % (x, hl)][:, :], T.onesb[:, :], [[-2, 64], [1000, 2]], A.is_equal, 0.0,
-                                      -x - 1000 * hl, 1))
-    e_xj = one(g.iota(T.xj[:, :], [[1, 32]], 513, 32, allow_small_or_imprecise_dtypes=True))
-    e_win0 = one(g.iota(T.win[:, 0:512], [[0, 512]], 0, 0, allow_small_or_imprecise_dtypes=True))
-    e_mn0 = one(g.iota(T.mn[:, :], [[0, 512]], 0, 0))
-    w("Y", e_mn0)
-    e_mn = one(Y.dma_start(T.mn[0::16, :], T["me"][0:1, :]), 16)
-    w("g", e_onesf)
-    e_ax = ev()
-    inc(e_ax, g.affine_select(T.ax0[:, :], T.onesf[:, :], [[-32, 4], [0, 2], [-1, 16]], A.is_equal, 0.0, 0, 1))
-    inc(e_ax, g.affine_select(T.ax1[:, :], T.onesf[:, :], [[-32, 4], [0, 2], [-1, 16]], A.is_equal, 0.0, -16, 1))
-    w("g", e_sel20)
-    e_s2a = one(g.affine_select(T.sel2[:, :], T.sel2[:, :], [[-32, 4], [-1, 16]], A.not_equal, 1.0, 0, 1))
-    e_ml = one(g.iota(T.ml[:, :], [[1, 32]], 0, 32))
-    w("g", e_s2a)
-    e_sel2 = one(g.affine_select(T.sel2[:, :], T.sel2[:, :], [[-32, 4], [-1, 16]], A.not_equal, 1.0, -16, 1))
-    e_prm = one(g.affine_select(T.prm[:, :], T.onesf[:, :], [[-16, 2], [-1, 16], [-32, 4]], A.is_equal, 0.0, 0, 1))
-    e_mw0 = one(g.iota(T.mwin[:, 0:512], [[0, 512]], 0, 0, allow_small_or_imprecise_dtypes=True))
 
     P.wait_ge(T.sem.x1, n1)
     w("P", e_pall)
@@ -272,6 +332,15 @@ def rank_program(g, core, T, topo):
         for m in range(n):
             inc(e, mm(bank[:, 128 * m:128 * m + 128], T.sm[:, 128 * (k + m):128 * (k + m) + 128], T.o1[:, :]))
         qn = "VSVSV"[j]
+        if j == 0:
+            e_vl = one(V.tensor_scalar(T.vl[:, :], T.vr[:, :], 127, None, A.bitwise_and))
+            w("V", e_ml)
+            e_ml2 = one(V.tensor_scalar(T.ml2[:, :], T.ml[:, :], 511, None, A.bitwise_and))
+        if j == 2:
+            w("V", e_vl, e_ml2)
+            for h in range(2):
+                inc(e_hl, V.tensor_scalar(T.hl1[:, 128 * h:128 * h + 128], T.vl[:, h::2], 1.0, None, A.add))
+            e_ml16 = one(V.tensor_copy(T.ml16[:, :], T.ml2[:, :]))
         w(qn, e)
         inc(e_w8, copy(qn, T.win8[:, 128 * k:128 * (k + n)], bank[:, 0:128 * n]))
         k += n
@@ -292,33 +361,34 @@ def rank_program(g, core, T, topo):
             inc(e_vp, mm(out, T["lh%d1" % x][:, :], T.hl1[:, 128 * h:128 * h + 128], False, True))
     w("S", e_vp)
     e_vb = one(S.activation(T.vb[:, :], T.p2[:, :], Fn.Copy))
+    w("S", e_ml16, e_mn)
+    e_mv = one(S.activation(T.mv[:, :], T.mn[:, :].indirect(T.ml16[:, 0:32]), Fn.Copy))
 
     w("P", e_qs, e_rt)
-    e_ns = ev()
+    e_tt = ev()
     for h in range(2):
         bank = (T.p1, T.p6)[h]
         w("P", e_g[h])
         e = ev()
         for p in range(16):
-            inc(e, mm(bank[:, p:128:16], T.gw[:, 2048 * h + p:2048 * h + 2048:16], T.qs[:, :]))
+            inc(e, mm(bank[:, 8 * p:8 * p + 8], T.gw[:, 2048 * h + p:2048 * h + 2048:16], T.qs[:, :]))
         w("V", e, e_rt)
-        u, v, t, s = T["u%d" % h], T["v%d" % h], T["t%d" % h], T["s%d" % h]
+        u, v = T["u%d" % h], T["v%d" % h]
         e = one(V.tensor_tensor(u[:, :], bank[:, 0:128], T.rt[:, 128 * h:128 * h + 128], A.mult))
         w("V", e)
         e = one(V.tensor_scalar(v[:, :], u[:, :], 7, 1, A.logical_shift_right, A.bitwise_and))
         w("V", e)
-        e = one(V.tensor_tensor(t[:, :], v[:, 0:64], v[:, 64:128], A.max))
-        w("V", e)
-        e = one(V.tensor_tensor(s[:, :], t[:, 0:32], t[:, 32:64], A.max))
-        w("V", e)
-        inc(e_ns, V.tensor_tensor(T.ns[:, 16 * h:16 * h + 16], s[:, 0:16], s[:, 16:32], A.max))
+        inc(e_tt, V.tensor_tensor(T.tt[:, 64 * h:64 * h + 64], v[:, 0::2], v[:, 1::2], A.max))
+    w("V", e_tt, e_msk)
+    e_ns = one(V.tensor_tensor_scan(T.sc[:, :], T.msk[:, :], T.tt[:, :], 0.0, A.mult, A.max))
+    ns = T.sc[:, 3:128:4]
 
     w("V", e_ns, e_onesb)
-    e_cum = one(V.tensor_tensor_scan(T.cum[:, :], T.ns[:, :], T.onesb[:, 0:32], 0.0, A.add, A.subtract))
+    e_cum = one(V.tensor_tensor_scan(T.cum[:, :], ns, T.onesb[:, 0:32], 0.0, A.add, A.subtract))
     w("P", e_cum, e_tri)
     e_base = one(mm(T.p0[:, 16:17], T.tri[:, :], T.cum[:, 31:32]))
     w("V", e_xj)
-    e_e1 = one(V.tensor_tensor(T.e1[:, :], T.ns[:, :], T.xj[:, :], A.mult))
+    e_e1 = one(V.tensor_tensor(T.e1[:, :], ns, T.xj[:, :], A.mult))
     w("V", e_cum, e_e1)
     e_e2 = one(V.tensor_tensor(T.e2[:, :], T.e1[:, :], T.cum[:, :], A.subtract))
     w("V", e_base, e_e2)
@@ -330,98 +400,79 @@ def rank_program(g, core, T, topo):
     for b in range(4):
         inc(e_ls, mm(T.p6[:, 128 + b:160:4], T.win[:, b:512:4], T.sel[:, :]))
     w("V", e_ls)
-    e_z = one(V.tensor_copy(T.z[:, :], T.p6[:, 128:160]))
-    w("V", e_z)
-    slot2 = T.rx2[:, 4 * me:4 * me + 4]
-    e_own2 = one(V.tensor_copy(slot2, T.z[:, 4 * me:4 * me + 4]))
+    e_z = one(V.tensor_copy(T.z16[:, :], T.p6[:, 128:160]))
+    e_own2 = one(V.tensor_copy(T.offo[:, 0:4], T.p6[:, 128 + 4 * me:132 + 4 * me]))
 
     w("g", e_z)
-    m2 = send(x2, lambda r: T.sem.x2, T.sem.l2, lambda r: T.z[:, 4 * r:4 * r + 4], lambda r: slot2)
+
+    def land2(r):
+        k = slot_of(r, me, T, topo)
+        return T.off2[:, 4 * k:4 * k + 4]
+    m2 = send(x2, lambda r: T.sem.x2, T.sem.l2, lambda r: T.z16[:, 4 * r:4 * r + 4], land2)
 
     w("P", e_negb)
-    e_cnt = one(mm(T.p7[0:64, 128:129], T.negb[:, :], T.cum[:, 31:32]))
-    w("V", e_ml)
-    e_ml2 = one(V.tensor_scalar(T.ml2[:, :], T.ml[:, :], 511, None, A.bitwise_and))
-    e_sg = one(V.tensor_scalar(T.sg[:, :], T.gi[:, :], 1, None, A.bitwise_and))
-    w("V", e_ml2)
-    e_ml16 = one(V.tensor_copy(T.ml16[:, :], T.ml2[:, :]))
-    w("V", e_sg)
-    e_sgf = one(V.tensor_scalar(T.sgf[:, :], T.sg[:, :], float(HALF), None, A.mult))
-    w("S", e_ml16, e_mn)
-    e_mv = one(S.activation(T.mv[:, :], T.mn[:, :].indirect(T.ml16[:, 0:32]), Fn.Copy))
-    e_b70 = one(V.memset(T.b7[:, :], 0.0))
-    w("V", e_b70)
-    e_b7 = one(V.tensor_scalar(T.b7[:, 48:64], T.onesf[:, 0:16], T.m16f[:, 0:1], None, A.mult))
+    e_cnt = one(mm(T.p7[:, 128:129], T.negb[:, :], T.cum[:, 31:32]))
+    w("S", e_cnt)
+    e_yc = one(S.activation(T.yo[:, 64:65], T.p7[:, 128:129], Fn.Copy))
+    w("V", e_mv, e_mw0)
+    e_ms1 = one(V.tensor_copy(T.mwin[:, 0:WIN].indirect(T.off[:, 0:24]), T.mv[:, 0:384]))
+    window = T.at2[:, 0:16392]
+    w("S", e_own2, e_at)
+    S.wait_ge(T.sem.wn, nw)
+    e_own3 = one(copy("S", T.ga[:, 448:512], window.indirect(T.offo[:, 0:4])))
 
-    P.wait_ge(T.sem.x2, n2)
-    w("P", e_own2, e_ax)
-    e_tb = ev()
-    for xx in range(2):
-        inc(e_tb, mm(T.p0[:, 64 + xx:128:2], T["ax%d" % xx][:, :], T.rx2[:, :]))
-    w("V", e_tb, e_sgf)
-    e_off2 = one(V.tensor_scalar(T.off2[:, :], T.p0[:, 64:128], T.sgf[:, 0:1], float(HALF + 1), A.subtract, A.min))
-    w("V", e_off2, e_at)
-    w("S", e_off2, e_at)
+    V.wait_ge(T.sem.wn, nw)
+    w("V", e_at)
     e_ga = []
-    for k, (ch, rs) in enumerate(order):
-        r0 = rs[0]
-        src = T.at2[:, 0:HALF + 8].indirect(T.off2[:, 8 * r0:8 * r0 + 16])
-        e_ga.append(one(copy("VS"[k % 2], T.ga[:, 128 * r0:128 * r0 + 256], src)))
-    w("P", e_sel2, e_vb)
-    e_zs = []
-    slot3 = T.rx3[:, 448:512]
-    e_own3 = ev()
-    for k, (ch, rs) in enumerate(order):
-        bank = T["p%d" % (2 + k)]
-        w("P", e_ga[k])
-        e = ev()
-        for j, r in enumerate(rs):
-            inc(e, mm(bank[:, 64 * j:64 * j + 64], T.ga[:, 128 * r:128 * r + 128], T.sel2[:, :]))
-        qn = "VS"[k % 2]
-        w(qn, e)
-        e_zs.append(ev())
-        for j, r in enumerate(rs):
-            if r == me:
-                inc(e_own3, copy(qn, slot3, bank[:, 64 * j:64 * j + 64]))
-            else:
-                inc(e_zs[k], copy(qn, T.zs[:, 64 * r:64 * r + 64], bank[:, 64 * j:64 * j + 64]))
+    for qn in "VS":
+        names[qn].wait_ge(T.sem.x2, n2)
+    for qn, k, n in (("V", 0, 2), ("S", 2, 2), ("V", 4, 2), ("S", 6, 1)):
+        e_ga.append(one(copy(qn, T.ga[:, 64 * k:64 * (k + n)], window.indirect(T.off2[:, 4 * k:4 * (k + n)]))))
 
     def land3(r):
         k = slot_of(r, me, T, topo)
         return T.rx3[:, 64 * k:64 * k + 64]
+
+    def block(r):
+        k = slot_of(me, r, T, topo)
+        return T.ga[:, 64 * k:64 * k + 64]
     m3 = 0
     for k, call in enumerate(x3):
-        w("g", e_zs[k])
-        m3 += send([call], lambda r: T.sem.x3a if slot_of(r, me, T, topo) < 4 else T.sem.x3b, T.sem.l3,
-                   lambda r: T.zs[:, 64 * r:64 * r + 64], land3)
+        w("g", e_ga[2 * k], e_ga[2 * k + 1])
+        m3 += send([call], lambda r: T.sem.x3a if slot_of(r, me, T, topo) < 4 else T.sem.x3b, T.sem.l3, block, land3)
 
-    w("V", e_mv, e_mw0, e_off)
-    e_ms = one(V.tensor_copy(T.mwin[:, 0:WIN].indirect(T.off[:, 0:32]), T.mv[:, :]))
-    w("P", e_ms, e_b7, e_cnt)
-    for k in range(4):
-        mm(T.p7[0:64, 0:128], T.b7[:, 48 - 16 * k:112 - 16 * k], T.mwin[:, 128 * k:128 * k + 128], k == 0, False)
+    w("V", e_ms1)
+    e_ms = one(V.tensor_copy(T.mwin[:, 0:WIN].indirect(T.off[:, 24:32]), T.mv[:, 384:512]))
+    w("P", e_ms, e_b7, e_w8)
+    for k in range(8):
+        e = mm(T.p5[:, 0:64], T.b7[:, 112 - 16 * k:240 - 16 * k], T.mwin[:, 64 * k:64 * k + 64], k == 0, k == 7)
+    e_mm = one(e)
+    w("V", e_mm, e_own3)
+    e_qm = ev()
+    for v in range(4):
+        inc(e_qm, V.tensor_tensor(T.qm[:, 16 * v:16 * v + 16], T.p5[:, v:64:4],
+                                  T.ga[:, 448 + 16 * v:464 + 16 * v], A.add))
 
     V.wait_ge(T.sem.x3a, n3a)
     e = one(V.tensor_tensor(T.q1[:, :], T.rx3[:, 0:128], T.rx3[:, 128:256], A.add))
     w("V", e)
     e = one(V.tensor_tensor(T.q2[:, :], T.q1[:, 0:64], T.q1[:, 64:128], A.add))
-    w("P", e, e_prm)
-    mm(T.p7[0:64, 0:128], T.q2[:, :], T.prm[:, :], False, False)
+    w("V", e, e_qm)
+    e = one(V.tensor_tensor(T.rx3[:, 448:512], T.q2[:, :], T.qm[:, :], A.add))
     V.wait_ge(T.sem.x3b, n3b)
-    w("V", e_own3)
+    w("V", e)
     e = one(V.tensor_tensor(T.q3[:, :], T.rx3[:, 256:384], T.rx3[:, 384:512], A.add))
     w("V", e)
-    e = one(V.tensor_tensor(T.q4[:, :], T.q3[:, 0:64], T.q3[:, 64:128], A.add))
-    w("P", e)
-    e_fin = one(mm(T.p7[0:64, 0:128], T.q4[:, :], T.prm[:, :], False, True))
-    w("V", e_fin)
-    e_yo = one(V.tensor_copy(T.yo[:, :], T.p7[0:64, 0:129]))
+    e_yo = ev()
+    for v in range(4):
+        inc(e_yo, V.tensor_tensor(T.yo[:, v:64:4], T.q3[:, 16 * v:16 * v + 16], T.q3[:, 64 + 16 * v:80 + 16 * v], A.add))
     e_y = ev()
-    for k in range(4):
+    for k in range(8):
         qn = "YS"[k % 2]
-        n = 129 if k == 3 else 128
-        w(qn, e_yo)
-        inc(e_y, names[qn].dma_start(T.y[:, 128 * k:128 * k + n], T.yo[16 * k:16 * k + 16, 0:n]), 16)
+        n = 65 if k == 7 else 64
+        w(qn, e_yo, e_yc)
+        inc(e_y, names[qn].dma_start(T.y[:, 64 * k:64 * k + n], T.yo[16 * k:16 * k + 16, 0:n]), 16)
+    g.wait_ge(T.sem.l0, m0)
     g.wait_ge(T.sem.l1, m1)
     g.wait_ge(T.sem.l2, m2)
     g.wait_ge(T.sem.l3, m3)

@@ -5,16 +5,16 @@ from concourse.mybir import AluOpType as A, ActivationFunctionType as Fn
 F32, BF, I32, U16 = "float32", "bfloat16", "int32", "uint16"
 WIN = 5120
 ROWS = 16384
-PARTS = (2816, 2304, 2304)
+PARTS = (1920, 1792, 1792)
 OWN = ROWS - sum(PARTS)
 SCRATCH = {}
 for _t, _list in (
-        (BF, "f1 128,f2 128,pall 128,o1 128,onesb 128,negb 128,m16 16,gp 1,wp 16,bd 128,sm 2048,idb 128,tri 128,qs 8,"
-             "bb 256,rb 256,vb 512,win8 2048,gw 4096,tt 128,sc 128,msk 128,cum 32,win 5120,sel 8,selh 8,"
+        (BF, "f1 128,f2 128,pall 136,onesb 128,negb 128,m16 16,wp 16,idb 128,tri 128,qs0 8,qs 8,"
+             "bb 256,rb 256,vb 512,win8 1024,gw 4096,tt 128,sc 128,msk 128,cum 32,win 5120,sel 8,selh 8,"
              "lh00 128,lh01 128,lh10 128,lh11 128,hl0 256,hl1 256"),
-        (I32, "a0 128,im 16,im2 16,gi 1,ib 128,ib2 128,fks 256,wi 256,bi 256,u0 128,u1 128,v0 128,v1 128,mn 512,"
-              "ml 32,ml2 32,at2 16392,vr 256,vh 256,vl 256,hw 2816"),
-        (F32, "onesf 128,m16f 16,gf 1,gpf 1,xj 32,rt 256,e1 32,e2 32,ga 512,rx3 512,q1 128,q2 64,q3 128,qm 64,"
+        (I32, "a0 128,im 16,im2 16,im8 8,gi 1,fks 256,wi 256,bi 256,u0 128,u1 128,v0 128,v1 128,mn 512,"
+              "ml 32,ml2 32,at2 16392,vr 256,vh 256,vl 256,hw 1920"),
+        (F32, "onesf 128,m8f 8,gf 1,gpf 1,xj 32,rt 256,e1 32,e2 32,ga 512,rx3 448,q1 128,q2 64,q3 64,qm 64,qf 64,qg 64,"
               "mv 512,mwin 5120,b7 240,yo 68"),
         (U16, "w16 256,off 32,off2 32,offo 8,ml16 32,z16 32")):
     for _x in _list.split(","):
@@ -26,7 +26,7 @@ SCRATCH["lm"] = ("sbuf", [1, 2], I32)
 SCRATCH["lf"] = ("sbuf", [1, 2], F32)
 for _k in range(8):
     SCRATCH["p%d" % _k] = ("psum", [128, 512], F32)
-SEMAPHORES = ["x1", "x2", "x3a", "x3b", "l0", "l1", "l2", "l3", "hr", "wn"] + ["e%d" % k for k in range(130)]
+SEMAPHORES = ["x1", "x2", "x3a", "x3b", "x3c", "l0", "l1", "l2", "l3", "hr", "wn"] + ["e%d" % k for k in range(130)]
 
 
 def helpers(core, T, topo):
@@ -36,13 +36,6 @@ def helpers(core, T, topo):
 
 def part_start(i, t=0):
     return 1 + OWN + sum(PARTS[:i]) + t * PARTS[i] // 2
-
-
-def helper_engines(core, T, topo):
-    hs = helpers(core, T, topo)
-    e = topo.engines(core, hs[0])
-    h, q = len(e) // 2, len(e) // 4
-    return [[e[:h], e[h:]], [e[:q], e[q:2 * q]], [e[2 * q:3 * q], e[3 * q:]]]
 
 
 def distance_order(core, T, topo):
@@ -69,13 +62,25 @@ def slot_of(rank, sender, T, topo):
     return flat.index(sender)
 
 
+def engine_sets(core, T, topo):
+    me = T.rank_of(core)
+    order = distance_order(core, T, topo)
+    near = [r for r in order[-1][1] if r != me]
+    eo = topo.engines(core, T.cores[order[0][1][0]])
+    return eo, [e for e in topo.engines(core, T.cores[near[0]]) if e not in eo]
+
+
+def helper_engines(core, T, topo):
+    eo, en = engine_sets(core, T, topo)
+    return [[eo, en], [eo[:4], eo[4:]], [en[:4], en[4:]]]
+
+
 def plans(core, T, topo):
     me = T.rank_of(core)
     order = distance_order(core, T, topo)
     far = [r for ch, rs in order[:-1] for r in rs]
     near = [r for r in order[-1][1] if r != me]
-    eo = topo.engines(core, T.cores[far[0]])
-    en = [e for e in topo.engines(core, T.cores[near[0]]) if e not in eo]
+    eo, en = engine_sets(core, T, topo)
     x1 = [[(far, eo), (near, en[:2])]]
     x2 = [[([far[k]], eo[2 * k:2 * k + 2]) for k in range(4)] + [(near, en[:2])],
           [([far[4 + k]], eo[4 * k:4 * k + 4]) for k in range(2)]]
@@ -164,7 +169,7 @@ def rank_program(g, core, T, topo):
 
     order, x1, x2, x3 = plans(core, T, topo)
     n1, n2 = arriving(core, T, topo, 1), arriving(core, T, topo, 2)
-    n3a, n3b = arriving(core, T, topo, 3, range(4)), arriving(core, T, topo, 3, range(4, 8))
+    n3a, n3b, n3c = [arriving(core, T, topo, 3, s) for s in (range(4), range(4, 6), range(6, 8))]
     hs, heng = helpers(core, T, topo), helper_engines(core, T, topo)
     nw = sum(2 * len(topo.engines(h, core)) for h in hs)
     m0 = sum(len(e) for h in heng for e in h)
@@ -202,38 +207,35 @@ def rank_program(g, core, T, topo):
     e_raw += [raw_load(Y, 1), raw_load(Y, 2)]
 
     e_im = one(g.iota(T.im[:, :], [[-1, 16]], 0, 1))
+    e_ml = one(g.iota(T.ml[:, :], [[1, 32]], 0, 32))
     e_onesb = one(V.memset(T.onesb[:, :], 1.0))
     e_onesf = one(V.memset(T.onesf[:, :], 1.0))
-    e_ib = one(g.iota(T.ib[:, :], [[-16, 8], [0, 16]], 0, 1))
     w("V", e_im)
-    e_gi = one(V.tensor_scalar(T.gi[:, :], T.im[:, 0:1], 4, None, A.arith_shift_right))
-    e_im2 = one(V.tensor_scalar(T.im2[:, :], T.im[:, :], 15, None, A.bitwise_and))
+    e_gi = one(V.tensor_scalar(T.gi[:, :], T.im[:, 0:1], 3, 7, A.logical_shift_right, A.bitwise_and))
+    e_im8 = one(V.tensor_scalar(T.im8[:, :], T.im[:, 0:8], 7, None, A.bitwise_and))
     w("V", e_gi)
     e_gf = one(V.tensor_copy(T.gf[:, :], T.gi[:, :]))
+    w("S", e_gf)
+    e_gp = one(S.activation(T.gpf[:, :], T.gf[:, :], Fn.Exp, scale=math.log(2.0)))
+    e_im2 = one(V.tensor_scalar(T.im2[:, :], T.im[:, :], 15, None, A.bitwise_and))
+    w("V", e_im8)
+    e_m8f = one(V.tensor_scalar(T.m8f[:, :], T.im8[:, :], 0.0, None, A.is_equal))
+    e_wp = one(V.memset(T.wp[:, :], 0.0))
     w("V", e_im2)
     e_m16 = one(V.tensor_scalar(T.m16[:, :], T.im2[:, :], 0.0, None, A.is_equal))
-    w("S", e_gf)
-    e_gp = one(S.activation(T.gp[:, :], T.gf[:, :], Fn.Exp, scale=math.log(2.0)))
-    w("V", e_ib)
-    e_ib2 = one(V.tensor_scalar(T.ib2[:, :], T.ib[:, :], 4, None, A.arith_shift_right))
+    w("V", e_ml)
+    e_ml2 = one(V.tensor_scalar(T.ml2[:, :], T.ml[:, :], 511, None, A.bitwise_and))
+    e_pt = one(V.memset(T.pall[:, 128:136], 0.0))
     w("V", e_m16)
-    e_m16f = one(V.tensor_copy(T.m16f[:, :], T.m16[:, :]))
-    w("V", e_ib2)
-    e_bd = one(V.tensor_scalar(T.bd[:, :], T.ib2[:, :], 0.0, None, A.is_equal))
-    w("V", e_bd, e_m16f)
-    w("S", e_bd, e_m16f)
-    e_sm = ev()
-    for m in range(16):
-        out, col = T.sm[:, 128 * m:128 * m + 128], T.m16f[:, m:m + 1]
-        if m % 4 == 0:
-            inc(e_sm, V.tensor_scalar(out, T.bd[:, :], col, None, A.mult))
-        else:
-            inc(e_sm, S.activation(out, T.bd[:, :], Fn.Copy, scale=col))
+    e_selh = one(V.tensor_scalar(T.selh[:, :], T.m16[:, 0::2], 128.0, None, A.mult))
+    w("V", e_ml2)
+    e_ml16 = one(V.tensor_copy(T.ml16[:, :], T.ml2[:, :]))
+    w("V", e_selh)
+    e_sel = one(V.tensor_tensor(T.sel[:, :], T.selh[:, :], T.m16[:, 1::2], A.add))
+    e_slot = one(V.memset(T.at2[:, 0:1], 0))
     w("g", e_onesb)
     e_id = one(g.affine_select(T.idb[:, :], T.onesb[:, :], [[-1, 128]], A.is_equal, 0.0, 0, 1))
     e_tri = one(g.affine_select(T.tri[:, :], T.onesb[:, :], [[1, 128]], A.is_gt, 0.0, 0, -1))
-    e_qs = one(g.affine_select(T.qs[:, :], T.onesb[:, 0:8], [[-16, 8]], A.is_equal, 0.0, 0, 1))
-    e_ml = one(g.iota(T.ml[:, :], [[1, 32]], 0, 32))
 
     w("g", e_raw[0])
     send_raw([0])
@@ -242,10 +244,11 @@ def rank_program(g, core, T, topo):
     e_lf = one(V.tensor_copy(T.lf[:, :], T.lm[:, :]))
     w("P", e_lf, e_onesf)
     e_lp = one(mm(T.p0[:, 0:2], T.onesf[0:1, :], T.lf[:, :]))
-    w("V", e_gp)
-    e_gpf = one(V.tensor_copy(T.gpf[:, :], T.gp[:, :]))
-    w("V", e_gpf)
-    e_w = one(V.tensor_scalar(T.wp[:, :], T.m16[:, :], T.gpf[:, 0:1], None, A.mult))
+    w("V", e_wp, e_m8f, e_gp)
+    e_w = ev()
+    for x in range(2):
+        s = slice(64 * x, 64 * x + 64)
+        inc(e_w, V.tensor_scalar(T.wp[s, 8 * x:8 * x + 8], T.m8f[s, :], T.gpf[s, 0:1], None, A.mult))
     w("V", e_lp, e_a0)
     e_f1 = one(V.tensor_scalar(T.f1[:, :], T.a0[:, :], T.p0[:, 0:1], None, A.is_lt))
     e_f2 = one(V.tensor_scalar(T.f2[:, :], T.a0[:, :], T.p0[:, 1:2], None, A.is_gt))
@@ -256,7 +259,6 @@ def rank_program(g, core, T, topo):
     w("V", e_pk)
     slot1 = T.pall[:, 16 * me:16 * me + 16]
     e_pall = one(V.tensor_copy(slot1, T.p7[:, 0:16]))
-    e_slot = one(V.memset(T.at2[:, 0:1], 0))
 
     w("g", e_pall)
     m1 = send(x1, lambda r: T.sem.x1, T.sem.l1, lambda r: slot1, lambda r: slot1)
@@ -264,12 +266,15 @@ def rank_program(g, core, T, topo):
     send_raw([1, 2])
 
     e_mn0 = one(g.iota(T.mn[:, :], [[0, 512]], 0, 0))
-    e_msk = one(g.affine_select(T.msk[:, :], T.onesb[:, :], [[0, 32], [1, 4]], A.not_equal, 0.0, 0, 0))
+    e_qs0 = one(g.affine_select(T.qs0[:, :], T.onesb[:, 0:8], [[-16, 8]], A.is_equal, 0.0, 0, 1))
+    w("g", e_qs0)
+    e_qs = one(g.affine_select(T.qs[:, :], T.qs0[:, :], [[-16, 8]], A.not_equal, 256.0, -8, 1))
     e_lh = ev()
     for x in range(2):
         for hl in range(2):
             inc(e_lh, g.affine_select(T["lh%d%d" % (x, hl)][:, :], T.onesb[:, :], [[-2, 64], [1000, 2]], A.is_equal, 0.0,
                                       -x - 1000 * hl, 1))
+    e_msk = one(g.affine_select(T.msk[:, :], T.onesb[:, :], [[0, 32], [1, 4]], A.not_equal, 0.0, 0, 0))
     e_xj = one(g.iota(T.xj[:, :], [[1, 32]], 513, 32, allow_small_or_imprecise_dtypes=True))
     e_win0 = one(g.iota(T.win[:, 0:512], [[0, 512]], 0, 0, allow_small_or_imprecise_dtypes=True))
     e_mw0 = one(g.iota(T.mwin[:, 0:512], [[0, 512]], 0, 0, allow_small_or_imprecise_dtypes=True))
@@ -288,8 +293,8 @@ def rank_program(g, core, T, topo):
             e_mn = one(Y.dma_start(T.mn[0::16, :], T["me"][0:1, :]), 16)
 
     w("V", e_fk)
-    e_bi = one(V.tensor_scalar(T.bi[:, :], T.fks[:, :], 11, None, A.arith_shift_right))
-    e_wi = one(V.tensor_scalar(T.wi[:, :], T.fks[:, :], 2047, None, A.bitwise_and))
+    e_bi = one(V.tensor_scalar(T.bi[:, :], T.fks[:, :], 10, None, A.arith_shift_right))
+    e_wi = one(V.tensor_scalar(T.wi[:, :], T.fks[:, :], 1023, None, A.bitwise_and))
     w("V", e_bi)
     e_bb = ev()
     for h in range(2):
@@ -307,40 +312,29 @@ def rank_program(g, core, T, topo):
             inc(e_rp, mm(T.p1[:, 128 * h + d:128 * h + 128:8], T.rb[:, 128 * h:128 * h + 128],
                          T.idb[:, 16 * d:16 * d + 16]))
     w("S", e_rp)
-    e_rt = one(S.activation(T.rt[:, :], T.p1[:, 0:256], Fn.Copy, scale=128.0))
+    e_rt = one(S.activation(T.rt[:, :], T.p1[:, 0:256], Fn.Copy, scale=32768.0))
     w("V", e_vr)
     e_vh = one(V.tensor_scalar(T.vh[:, :], T.vr[:, :], 7, None, A.arith_shift_right))
-    e_selh = one(V.tensor_scalar(T.selh[:, :], T.m16[:, 0::2], 128.0, None, A.mult))
+    e_vl = one(V.tensor_scalar(T.vl[:, :], T.vr[:, :], 127, None, A.bitwise_and))
     e_hl = ev()
     w("V", e_vh)
     for h in range(2):
         inc(e_hl, V.tensor_copy(T.hl0[:, 128 * h:128 * h + 128], T.vh[:, h::2]))
-    w("V", e_selh)
-    e_sel = one(V.tensor_tensor(T.sel[:, :], T.selh[:, :], T.m16[:, 1::2], A.add))
 
     P.wait_ge(T.sem.x1, n1)
-    w("P", e_pall)
-    e_t1 = one(mm(T.p7[:, 128:256], T.pall[:, :], T.idb[:, :]))
-    w("V", e_t1)
-    e_o1 = one(V.tensor_copy(T.o1[:, :], T.p7[:, 128:256]))
-    w("P", e_o1, e_sm)
+    w("P", e_pall, e_pt)
     e_w8 = ev()
     k = 0
-    for j, n in enumerate((4, 4, 4, 2, 2)):
+    for j, n in enumerate((2, 2, 2, 1, 1)):
         bank = T["p%d" % (2 + j)]
         e = ev()
         for m in range(n):
-            inc(e, mm(bank[:, 128 * m:128 * m + 128], T.sm[:, 128 * (k + m):128 * (k + m) + 128], T.o1[:, :]))
+            inc(e, mm(bank[:, 128 * m:128 * m + 128], T.pall[:, k + m:k + m + 128], T.idb[:, :]))
         qn = "VSVSV"[j]
-        if j == 0:
-            e_vl = one(V.tensor_scalar(T.vl[:, :], T.vr[:, :], 127, None, A.bitwise_and))
-            w("V", e_ml)
-            e_ml2 = one(V.tensor_scalar(T.ml2[:, :], T.ml[:, :], 511, None, A.bitwise_and))
-        if j == 2:
-            w("V", e_vl, e_ml2)
-            for h in range(2):
-                inc(e_hl, V.tensor_scalar(T.hl1[:, 128 * h:128 * h + 128], T.vl[:, h::2], 1.0, None, A.add))
-            e_ml16 = one(V.tensor_copy(T.ml16[:, :], T.ml2[:, :]))
+        if j in (0, 2):
+            h = j // 2
+            w("V", e_vl)
+            inc(e_hl, V.tensor_scalar(T.hl1[:, 128 * h:128 * h + 128], T.vl[:, h::2], 1.0, None, A.add))
         w(qn, e)
         inc(e_w8, copy(qn, T.win8[:, 128 * k:128 * (k + n)], bank[:, 0:128 * n]))
         k += n
@@ -376,7 +370,7 @@ def rank_program(g, core, T, topo):
         u, v = T["u%d" % h], T["v%d" % h]
         e = one(V.tensor_tensor(u[:, :], bank[:, 0:128], T.rt[:, 128 * h:128 * h + 128], A.mult))
         w("V", e)
-        e = one(V.tensor_scalar(v[:, :], u[:, :], 7, 1, A.logical_shift_right, A.bitwise_and))
+        e = one(V.tensor_scalar(v[:, :], u[:, :], 15, 1, A.logical_shift_right, A.bitwise_and))
         w("V", e)
         inc(e_tt, V.tensor_tensor(T.tt[:, 64 * h:64 * h + 64], v[:, 0::2], v[:, 1::2], A.max))
     w("V", e_tt, e_msk)
@@ -433,13 +427,16 @@ def rank_program(g, core, T, topo):
         k = slot_of(r, me, T, topo)
         return T.rx3[:, 64 * k:64 * k + 64]
 
+    def sem3(r):
+        return (T.sem.x3a, T.sem.x3a, T.sem.x3b, T.sem.x3c)[slot_of(r, me, T, topo) // 2]
+
     def block(r):
         k = slot_of(me, r, T, topo)
         return T.ga[:, 64 * k:64 * k + 64]
     m3 = 0
     for k, call in enumerate(x3):
         w("g", e_ga[2 * k], e_ga[2 * k + 1])
-        m3 += send([call], lambda r: T.sem.x3a if slot_of(r, me, T, topo) < 4 else T.sem.x3b, T.sem.l3, block, land3)
+        m3 += send([call], sem3, T.sem.l3, block, land3)
 
     w("V", e_ms1)
     e_ms = one(V.tensor_copy(T.mwin[:, 0:WIN].indirect(T.off[:, 24:32]), T.mv[:, 384:512]))
@@ -458,14 +455,16 @@ def rank_program(g, core, T, topo):
     w("V", e)
     e = one(V.tensor_tensor(T.q2[:, :], T.q1[:, 0:64], T.q1[:, 64:128], A.add))
     w("V", e, e_qm)
-    e = one(V.tensor_tensor(T.rx3[:, 448:512], T.q2[:, :], T.qm[:, :], A.add))
+    e = one(V.tensor_tensor(T.qf[:, :], T.q2[:, :], T.qm[:, :], A.add))
+    V.wait_ge(T.sem.x3c, n3c)
+    w("V", e)
+    e_qg = one(V.tensor_tensor(T.qg[:, :], T.qf[:, :], T.rx3[:, 384:448], A.add))
     V.wait_ge(T.sem.x3b, n3b)
-    w("V", e)
-    e = one(V.tensor_tensor(T.q3[:, :], T.rx3[:, 256:384], T.rx3[:, 384:512], A.add))
-    w("V", e)
+    e = one(V.tensor_tensor(T.q3[:, :], T.rx3[:, 256:320], T.rx3[:, 320:384], A.add))
+    w("V", e, e_qg)
     e_yo = ev()
     for v in range(4):
-        inc(e_yo, V.tensor_tensor(T.yo[:, v:64:4], T.q3[:, 16 * v:16 * v + 16], T.q3[:, 64 + 16 * v:80 + 16 * v], A.add))
+        inc(e_yo, V.tensor_tensor(T.yo[:, v:64:4], T.q3[:, 16 * v:16 * v + 16], T.qg[:, 16 * v:16 * v + 16], A.add))
     e_y = ev()
     for k in range(8):
         qn = "YS"[k % 2]

import math
from concourse.bass import DstId, RemoteDMATransfer
from concourse.mybir import AluOpType as A, ActivationFunctionType as Fn

F32, BF, I32, U16 = "float32", "bfloat16", "int32", "uint16"
WIN = 5120
ROWS = 16384
PARTS = (1920, 1792, 1792)
OWN = ROWS - sum(PARTS)
SCRATCH = {}
for _t, _list in (
        (BF, "f1 128,f2 128,pall 136,onesb 128,negb 128,m16 16,wp 16,idb 128,tri 128,qs0 8,qs 8,"
             "bb 256,rb 256,vb 512,win8 1024,gw 4096,tt 128,sc 128,msk 128,cum 32,win 5120,sel 8,selh 8,"
             "lh00 128,lh01 128,lh10 128,lh11 128,hl0 256,hl1 256"),
        (I32, "a0 128,im 16,im2 16,im8 8,gi 1,fks 256,wi 256,bi 256,u0 128,u1 128,v0 128,v1 128,mn 512,"
              "ml 32,ml2 32,at2 16392,vr 256,vh 256,vl 256,hw 1920"),
        (F32, "onesf 128,m8f 8,gf 1,gpf 1,xj 32,rt 256,e1 32,e2 32,ga 512,rx3 448,q1 128,q2 64,q3 64,qm 64,qf 64,qg 64,"
              "mv 512,mwin 5120,b7 240,yo 68"),
        (U16, "w16 256,off 32,off2 32,offo 8,ml16 32,z16 32")):
    for _x in _list.split(","):
        SCRATCH[_x.split()[0]] = ("sbuf", [128, int(_x.split()[1])], _t)
for _k in range(3):
    SCRATCH["hd%d" % _k] = ("dram", [2, 128, PARTS[_k] // 16], I32)
    SCRATCH["raw%d" % _k] = ("sbuf", [128, PARTS[_k] // 8], I32)
SCRATCH["lm"] = ("sbuf", [1, 2], I32)
SCRATCH["lf"] = ("sbuf", [1, 2], F32)
for _k in range(8):
    SCRATCH["p%d" % _k] = ("psum", [128, 512], F32)
SEMAPHORES = ["x1", "x2", "x3a", "x3b", "x3c", "l0", "l1", "l2", "l3", "hr", "wn"] + ["e%d" % k for k in range(130)]


def helpers(core, T, topo):
    hs = [c for c in topo.cores_of(core) if c not in T.cores and topo.die(c) == topo.die(core)]
    return hs[:len(PARTS)]


def part_start(i, t=0):
    return 1 + OWN + sum(PARTS[:i]) + t * PARTS[i] // 2


def distance_order(core, T, topo):
    here = topo.chip(core)
    chips = []
    for c in T.cores:
        if topo.chip(c) not in chips:
            chips.append(topo.chip(c))

    def far(ch):
        if ch == here:
            return 0
        if topo.mates(ch, here):
            return 1
        return 2 if topo.same_plane(ch, here) else 3
    out = []
    for ch in sorted(chips, key=lambda ch: (-far(ch), (ch - here) % len(chips))):
        out.append((ch, [r for r in range(len(T.cores)) if topo.chip(T.cores[r]) == ch]))
    return out


def slot_of(rank, sender, T, topo):
    flat = [r for ch, rs in distance_order(T.cores[rank], T, topo) for r in rs if r != rank] + [rank]
    return flat.index(sender)


def engine_sets(core, T, topo):
    me = T.rank_of(core)
    order = distance_order(core, T, topo)
    near = [r for r in order[-1][1] if r != me]
    eo = topo.engines(core, T.cores[order[0][1][0]])
    return eo, [e for e in topo.engines(core, T.cores[near[0]]) if e not in eo]


def helper_engines(core, T, topo):
    eo, en = engine_sets(core, T, topo)
    return [[eo, en], [eo[:4], eo[4:]], [en[:4], en[4:]]]


def plans(core, T, topo):
    me = T.rank_of(core)
    order = distance_order(core, T, topo)
    far = [r for ch, rs in order[:-1] for r in rs]
    near = [r for r in order[-1][1] if r != me]
    eo, en = engine_sets(core, T, topo)
    x1 = [[(far, eo), (near, en[:2])]]
    x2 = [[([far[k]], eo[2 * k:2 * k + 2]) for k in range(4)] + [(near, en[:2])],
          [([far[4 + k]], eo[4 * k:4 * k + 4]) for k in range(2)]]
    x3 = [[([far[k]], eo[2 * k:2 * k + 2]) for k in range(4)],
          [([far[4 + k]], eo[4 * k:4 * k + 4]) for k in range(2)] + [(near, en[:4])]]
    return order, x1, x2, x3


def arriving(core, T, topo, which, slots=range(8)):
    me, n = T.rank_of(core), 0
    for c in T.cores:
        if c != core and slot_of(me, T.rank_of(c), T, topo) in slots:
            for call in plans(c, T, topo)[which]:
                for dests, eng in call:
                    if me in dests:
                        n += len(eng)
    return n


def transfer(dest_cores, eng, rsem, src, dst, topo):
    ids = []
    for c in dest_cores:
        rid, pid, se = topo.addr(c)
        ids.append(DstId(rid=rid, pnc=pid))
    return RemoteDMATransfer(dst_ids=ids, dma_engine_mask=sum(1 << e for e in eng), remote_sem=rsem, srcs=[src],
                             dsts=[dst] * len(ids))


def helper_program(g, core, T, topo):
    owners = [c for c in T.cores if core in helpers(c, T, topo)]
    if not owners:
        return
    owner = owners[0]
    i = helpers(owner, T, topo).index(core)
    n = PARTS[i] // 2
    for q in (g.sync, g.scalar):
        q.wait_ge(T.sem.hr, sum(len(e) for e in helper_engines(owner, T, topo)[i]))
    for t in range(2):
        for k in range(8):
            q = (g.sync, g.scalar)[k % 2]
            q.dma_start(T.hw[16 * k:16 * k + 16, n * t:n * t + n], T["hd%d" % i][t]).then_inc(T.sem["e%d" % t], 16)
    eng = topo.engines(core, owner)
    for t in range(2):
        g.wait_ge(T.sem["e%d" % t], 128)
        c0 = part_start(i, t)
        g.remote_dma_fused([transfer([owner], eng, T.sem.wn, T.hw[:, n * t:n * t + n], T.at2[:, c0:c0 + n], topo)],
                           local_sem=T.sem.l0)
    g.wait_ge(T.sem.l0, 2 * len(eng))


def rank_program(g, core, T, topo):
    me = T.rank_of(core)
    if me is None:
        helper_program(g, core, T, topo)
        return
    V, S, P, Y = g.vector, g.scalar, g.tensor, g.sync
    names = {"g": g, "V": V, "S": S, "P": P, "Y": Y}
    evs = []
    known = {k: [] for k in names}
    waited = []

    def ev():
        evs.append(0)
        return len(evs) - 1

    def inc(e, ins, n=1):
        ins.then_inc(T.sem["e%d" % e], n)
        evs[e] += n
        return e

    def one(ins, n=1):
        return inc(ev(), ins, n)

    def w(qn, *es):
        for e in es:
            if e not in known[qn]:
                names[qn].wait_ge(T.sem["e%d" % e], evs[e])
                known[qn].append(e)
                waited.append(e)

    def mm(out, lhsT, rhs, start=True, stop=True):
        return P.matmul(out, lhsT, rhs, start, stop)

    def copy(qn, out, in_):
        return V.tensor_copy(out, in_) if qn == "V" else S.activation(out, in_, Fn.Copy)

    order, x1, x2, x3 = plans(core, T, topo)
    n1, n2 = arriving(core, T, topo, 1), arriving(core, T, topo, 2)
    n3a, n3b, n3c = [arriving(core, T, topo, 3, s) for s in (range(4), range(4, 6), range(6, 8))]
    hs, heng = helpers(core, T, topo), helper_engines(core, T, topo)
    nw = sum(2 * len(topo.engines(h, core)) for h in hs)
    m0 = sum(len(e) for h in heng for e in h)

    def send(calls, rsem, lsem, src, dst):
        n = 0
        for call in calls:
            g.remote_dma_fused([transfer([T.cores[r] for r in dests], eng, rsem(dests[0]), src(dests[0]), dst(dests[0]),
                                         topo) for dests, eng in call], local_sem=lsem)
            n += sum(len(eng) for dests, eng in call)
        return n

    def raw(i, t):
        n = PARTS[i] // 16
        return T["raw%d" % i][:, n * t:n * t + n]

    def send_raw(which):
        g.remote_dma_fused([transfer([hs[i]], heng[i][t], T.sem.hr, raw(i, t), T["hd%d" % i][t], topo)
                            for i in which for t in range(2)], local_sem=T.sem.l0)

    def raw_load(q, i):
        e = ev()
        for t in range(2):
            c0 = part_start(i, t) - 1
            inc(e, q.dma_start(raw(i, t), T["at"][:, c0:c0 + PARTS[i] // 2]), 16)
        return e

    e_lim = one(S.dma_start(T.lm[:, :], T.lim[:, :]), 16)
    e_a0 = one(Y.dma_start(T.a0[:, :], T["at"][0:1, :]), 16)
    e_fk = one(S.dma_start(T.fks[:, :], T.fk[:, :]), 16)
    e_raw = [raw_load(Y, 0)]
    e_vr = ev()
    for k in range(8):
        inc(e_vr, Y.dma_start(T.vr[16 * k:16 * k + 16, :], T.fk[:, 32 * k:32 * k + 32]), 16)
    e_raw += [raw_load(Y, 1), raw_load(Y, 2)]

    e_im = one(g.iota(T.im[:, :], [[-1, 16]], 0, 1))
    e_ml = one(g.iota(T.ml[:, :], [[1, 32]], 0, 32))
    e_onesb = one(V.memset(T.onesb[:, :], 1.0))
    e_onesf = one(V.memset(T.onesf[:, :], 1.0))
    w("V", e_im)
    e_gi = one(V.tensor_scalar(T.gi[:, :], T.im[:, 0:1], 3, 7, A.logical_shift_right, A.bitwise_and))
    e_im8 = one(V.tensor_scalar(T.im8[:, :], T.im[:, 0:8], 7, None, A.bitwise_and))
    w("V", e_gi)
    e_gf = one(V.tensor_copy(T.gf[:, :], T.gi[:, :]))
    w("S", e_gf)
    e_gp = one(S.activation(T.gpf[:, :], T.gf[:, :], Fn.Exp, scale=math.log(2.0)))
    e_im2 = one(V.tensor_scalar(T.im2[:, :], T.im[:, :], 15, None, A.bitwise_and))
    w("V", e_im8)
    e_m8f = one(V.tensor_scalar(T.m8f[:, :], T.im8[:, :], 0.0, None, A.is_equal))
    e_wp = one(V.memset(T.wp[:, :], 0.0))
    w("V", e_im2)
    e_m16 = one(V.tensor_scalar(T.m16[:, :], T.im2[:, :], 0.0, None, A.is_equal))
    w("V", e_ml)
    e_ml2 = one(V.tensor_scalar(T.ml2[:, :], T.ml[:, :], 511, None, A.bitwise_and))
    e_pt = one(V.memset(T.pall[:, 128:136], 0.0))
    w("V", e_m16)
    e_selh = one(V.tensor_scalar(T.selh[:, :], T.m16[:, 0::2], 128.0, None, A.mult))
    w("V", e_ml2)
    e_ml16 = one(V.tensor_copy(T.ml16[:, :], T.ml2[:, :]))
    w("V", e_selh)
    e_sel = one(V.tensor_tensor(T.sel[:, :], T.selh[:, :], T.m16[:, 1::2], A.add))
    e_slot = one(V.memset(T.at2[:, 0:1], 0))
    w("g", e_onesb)
    e_id = one(g.affine_select(T.idb[:, :], T.onesb[:, :], [[-1, 128]], A.is_equal, 0.0, 0, 1))
    e_tri = one(g.affine_select(T.tri[:, :], T.onesb[:, :], [[1, 128]], A.is_gt, 0.0, 0, -1))

    w("g", e_raw[0])
    send_raw([0])

    w("V", e_lim)
    e_lf = one(V.tensor_copy(T.lf[:, :], T.lm[:, :]))
    w("P", e_lf, e_onesf)
    e_lp = one(mm(T.p0[:, 0:2], T.onesf[0:1, :], T.lf[:, :]))
    w("V", e_wp, e_m8f, e_gp)
    e_w = ev()
    for x in range(2):
        s = slice(64 * x, 64 * x + 64)
        inc(e_w, V.tensor_scalar(T.wp[s, 8 * x:8 * x + 8], T.m8f[s, :], T.gpf[s, 0:1], None, A.mult))
    w("V", e_lp, e_a0)
    e_f1 = one(V.tensor_scalar(T.f1[:, :], T.a0[:, :], T.p0[:, 0:1], None, A.is_lt))
    e_f2 = one(V.tensor_scalar(T.f2[:, :], T.a0[:, :], T.p0[:, 1:2], None, A.is_gt))
    w("P", e_w, e_f1)
    mm(T.p7[:, 0:16], T.f1[:, :], T.wp[:, :], True, False)
    w("P", e_f2)
    e_pk = one(mm(T.p7[:, 0:16], T.f2[:, :], T.wp[:, :], False, True))
    w("V", e_pk)
    slot1 = T.pall[:, 16 * me:16 * me + 16]
    e_pall = one(V.tensor_copy(slot1, T.p7[:, 0:16]))

    w("g", e_pall)
    m1 = send(x1, lambda r: T.sem.x1, T.sem.l1, lambda r: slot1, lambda r: slot1)
    w("g", e_raw[1], e_raw[2])
    send_raw([1, 2])

    e_mn0 = one(g.iota(T.mn[:, :], [[0, 512]], 0, 0))
    e_qs0 = one(g.affine_select(T.qs0[:, :], T.onesb[:, 0:8], [[-16, 8]], A.is_equal, 0.0, 0, 1))
    w("g", e_qs0)
    e_qs = one(g.affine_select(T.qs[:, :], T.qs0[:, :], [[-16, 8]], A.not_equal, 256.0, -8, 1))
    e_lh = ev()
    for x in range(2):
        for hl in range(2):
            inc(e_lh, g.affine_select(T["lh%d%d" % (x, hl)][:, :], T.onesb[:, :], [[-2, 64], [1000, 2]], A.is_equal, 0.0,
                                      -x - 1000 * hl, 1))
    e_msk = one(g.affine_select(T.msk[:, :], T.onesb[:, :], [[0, 32], [1, 4]], A.not_equal, 0.0, 0, 0))
    e_xj = one(g.iota(T.xj[:, :], [[1, 32]], 513, 32, allow_small_or_imprecise_dtypes=True))
    e_win0 = one(g.iota(T.win[:, 0:512], [[0, 512]], 0, 0, allow_small_or_imprecise_dtypes=True))
    e_mw0 = one(g.iota(T.mwin[:, 0:512], [[0, 512]], 0, 0, allow_small_or_imprecise_dtypes=True))
    e_negb = one(g.iota(T.negb[:, :], [[0, 128]], -1, 0, allow_small_or_imprecise_dtypes=True))
    e_b70 = one(g.iota(T.b7[:, :], [[0, 240]], 1, 0, allow_small_or_imprecise_dtypes=True))
    w("g", e_b70)
    e_b7 = one(g.affine_select(T.b7[:, :], T.b7[:, :], [[1, 15], [0, 16]], A.is_equal, 0.0, -7, 0))

    w("Y", e_slot)
    Y.wait_ge(T.sem.l1, m1)
    e_at = ev()
    for k in range(8):
        inc(e_at, Y.dma_start(T.at2[16 * k:16 * k + 16, 1:OWN + 1], T["at"][:, 0:OWN]), 16)
        if k == 3:
            w("Y", e_mn0)
            e_mn = one(Y.dma_start(T.mn[0::16, :], T["me"][0:1, :]), 16)

    w("V", e_fk)
    e_bi = one(V.tensor_scalar(T.bi[:, :], T.fks[:, :], 10, None, A.arith_shift_right))
    e_wi = one(V.tensor_scalar(T.wi[:, :], T.fks[:, :], 1023, None, A.bitwise_and))
    w("V", e_bi)
    e_bb = ev()
    for h in range(2):
        inc(e_bb, V.tensor_copy(T.bb[:, 128 * h:128 * h + 128], T.bi[:, h::2]))
    w("V", e_wi)
    e_w16 = ev()
    for h in range(2):
        inc(e_w16, V.tensor_copy(T.w16[:, 128 * h:128 * h + 128], T.wi[:, h::2]))
    w("S", e_bb)
    e_rb = one(S.activation(T.rb[:, :], T.bb[:, :], Fn.Exp, scale=-math.log(2.0)))
    w("P", e_rb, e_id)
    e_rp = ev()
    for h in range(2):
        for d in range(8):
            inc(e_rp, mm(T.p1[:, 128 * h + d:128 * h + 128:8], T.rb[:, 128 * h:128 * h + 128],
                         T.idb[:, 16 * d:16 * d + 16]))
    w("S", e_rp)
    e_rt = one(S.activation(T.rt[:, :], T.p1[:, 0:256], Fn.Copy, scale=32768.0))
    w("V", e_vr)
    e_vh = one(V.tensor_scalar(T.vh[:, :], T.vr[:, :], 7, None, A.arith_shift_right))
    e_vl = one(V.tensor_scalar(T.vl[:, :], T.vr[:, :], 127, None, A.bitwise_and))
    e_hl = ev()
    w("V", e_vh)
    for h in range(2):
        inc(e_hl, V.tensor_copy(T.hl0[:, 128 * h:128 * h + 128], T.vh[:, h::2]))

    P.wait_ge(T.sem.x1, n1)
    w("P", e_pall, e_pt)
    e_w8 = ev()
    k = 0
    for j, n in enumerate((2, 2, 2, 1, 1)):
        bank = T["p%d" % (2 + j)]
        e = ev()
        for m in range(n):
            inc(e, mm(bank[:, 128 * m:128 * m + 128], T.pall[:, k + m:k + m + 128], T.idb[:, :]))
        qn = "VSVSV"[j]
        if j in (0, 2):
            h = j // 2
            w("V", e_vl)
            inc(e_hl, V.tensor_scalar(T.hl1[:, 128 * h:128 * h + 128], T.vl[:, h::2], 1.0, None, A.add))
        w(qn, e)
        inc(e_w8, copy(qn, T.win8[:, 128 * k:128 * (k + n)], bank[:, 0:128 * n]))
        k += n
    w("V", e_w8, e_w16)
    w("S", e_w8, e_w16)
    e_g = [ev(), ev()]
    for h in range(2):
        for half in range(2):
            k = 2 * h + half
            src = T.win8[:, :].indirect(T.w16[:, 64 * k:64 * k + 64])
            inc(e_g[h], copy("VS"[half], T.gw[:, 1024 * k:1024 * k + 1024], src))
    w("P", e_hl, e_lh, e_w8)
    e_vp = ev()
    for h in range(2):
        for x in range(2):
            out = T.p2[:, 256 * h + 128 * x:256 * h + 128 * x + 128]
            mm(out, T["lh%d0" % x][:, :], T.hl0[:, 128 * h:128 * h + 128], True, False)
            inc(e_vp, mm(out, T["lh%d1" % x][:, :], T.hl1[:, 128 * h:128 * h + 128], False, True))
    w("S", e_vp)
    e_vb = one(S.activation(T.vb[:, :], T.p2[:, :], Fn.Copy))
    w("S", e_ml16, e_mn)
    e_mv = one(S.activation(T.mv[:, :], T.mn[:, :].indirect(T.ml16[:, 0:32]), Fn.Copy))

    w("P", e_qs, e_rt)
    e_tt = ev()
    for h in range(2):
        bank = (T.p1, T.p6)[h]
        w("P", e_g[h])
        e = ev()
        for p in range(16):
            inc(e, mm(bank[:, 8 * p:8 * p + 8], T.gw[:, 2048 * h + p:2048 * h + 2048:16], T.qs[:, :]))
        w("V", e, e_rt)
        u, v = T["u%d" % h], T["v%d" % h]
        e = one(V.tensor_tensor(u[:, :], bank[:, 0:128], T.rt[:, 128 * h:128 * h + 128], A.mult))
        w("V", e)
        e = one(V.tensor_scalar(v[:, :], u[:, :], 15, 1, A.logical_shift_right, A.bitwise_and))
        w("V", e)
        inc(e_tt, V.tensor_tensor(T.tt[:, 64 * h:64 * h + 64], v[:, 0::2], v[:, 1::2], A.max))
    w("V", e_tt, e_msk)
    e_ns = one(V.tensor_tensor_scan(T.sc[:, :], T.msk[:, :], T.tt[:, :], 0.0, A.mult, A.max))
    ns = T.sc[:, 3:128:4]

    w("V", e_ns, e_onesb)
    e_cum = one(V.tensor_tensor_scan(T.cum[:, :], ns, T.onesb[:, 0:32], 0.0, A.add, A.subtract))
    w("P", e_cum, e_tri)
    e_base = one(mm(T.p0[:, 16:17], T.tri[:, :], T.cum[:, 31:32]))
    w("V", e_xj)
    e_e1 = one(V.tensor_tensor(T.e1[:, :], ns, T.xj[:, :], A.mult))
    w("V", e_cum, e_e1)
    e_e2 = one(V.tensor_tensor(T.e2[:, :], T.e1[:, :], T.cum[:, :], A.subtract))
    w("V", e_base, e_e2)
    e_off = one(V.tensor_scalar(T.off[:, :], T.e2[:, :], T.p0[:, 16:17], 1.0, A.subtract, A.subtract))
    w("V", e_off, e_vb, e_win0)
    e_sc = one(V.tensor_copy(T.win[:, 0:WIN].indirect(T.off[:, 0:32]), T.vb[:, :]))
    w("P", e_sc, e_sel, e_ns)
    e_ls = ev()
    for b in range(4):
        inc(e_ls, mm(T.p6[:, 128 + b:160:4], T.win[:, b:512:4], T.sel[:, :]))
    w("V", e_ls)
    e_z = one(V.tensor_copy(T.z16[:, :], T.p6[:, 128:160]))
    e_own2 = one(V.tensor_copy(T.offo[:, 0:4], T.p6[:, 128 + 4 * me:132 + 4 * me]))

    w("g", e_z)

    def land2(r):
        k = slot_of(r, me, T, topo)
        return T.off2[:, 4 * k:4 * k + 4]
    m2 = send(x2, lambda r: T.sem.x2, T.sem.l2, lambda r: T.z16[:, 4 * r:4 * r + 4], land2)

    w("P", e_negb)
    e_cnt = one(mm(T.p7[:, 128:129], T.negb[:, :], T.cum[:, 31:32]))
    w("S", e_cnt)
    e_yc = one(S.activation(T.yo[:, 64:65], T.p7[:, 128:129], Fn.Copy))
    w("V", e_mv, e_mw0)
    e_ms1 = one(V.tensor_copy(T.mwin[:, 0:WIN].indirect(T.off[:, 0:24]), T.mv[:, 0:384]))
    window = T.at2[:, 0:16392]
    w("S", e_own2, e_at)
    S.wait_ge(T.sem.wn, nw)
    e_own3 = one(copy("S", T.ga[:, 448:512], window.indirect(T.offo[:, 0:4])))

    V.wait_ge(T.sem.wn, nw)
    w("V", e_at)
    e_ga = []
    for qn in "VS":
        names[qn].wait_ge(T.sem.x2, n2)
    for qn, k, n in (("V", 0, 2), ("S", 2, 2), ("V", 4, 2), ("S", 6, 1)):
        e_ga.append(one(copy(qn, T.ga[:, 64 * k:64 * (k + n)], window.indirect(T.off2[:, 4 * k:4 * (k + n)]))))

    def land3(r):
        k = slot_of(r, me, T, topo)
        return T.rx3[:, 64 * k:64 * k + 64]

    def sem3(r):
        return (T.sem.x3a, T.sem.x3a, T.sem.x3b, T.sem.x3c)[slot_of(r, me, T, topo) // 2]

    def block(r):
        k = slot_of(me, r, T, topo)
        return T.ga[:, 64 * k:64 * k + 64]
    m3 = 0
    for k, call in enumerate(x3):
        w("g", e_ga[2 * k], e_ga[2 * k + 1])
        m3 += send([call], sem3, T.sem.l3, block, land3)

    w("V", e_ms1)
    e_ms = one(V.tensor_copy(T.mwin[:, 0:WIN].indirect(T.off[:, 24:32]), T.mv[:, 384:512]))
    w("P", e_ms, e_b7, e_w8)
    for k in range(8):
        e = mm(T.p5[:, 0:64], T.b7[:, 112 - 16 * k:240 - 16 * k], T.mwin[:, 64 * k:64 * k + 64], k == 0, k == 7)
    e_mm = one(e)
    w("V", e_mm, e_own3)
    e_qm = ev()
    for v in range(4):
        inc(e_qm, V.tensor_tensor(T.qm[:, 16 * v:16 * v + 16], T.p5[:, v:64:4],
                                  T.ga[:, 448 + 16 * v:464 + 16 * v], A.add))

    V.wait_ge(T.sem.x3a, n3a)
    e = one(V.tensor_tensor(T.q1[:, :], T.rx3[:, 0:128], T.rx3[:, 128:256], A.add))
    w("V", e)
    e = one(V.tensor_tensor(T.q2[:, :], T.q1[:, 0:64], T.q1[:, 64:128], A.add))
    w("V", e, e_qm)
    e = one(V.tensor_tensor(T.qf[:, :], T.q2[:, :], T.qm[:, :], A.add))
    V.wait_ge(T.sem.x3c, n3c)
    w("V", e)
    e_qg = one(V.tensor_tensor(T.qg[:, :], T.qf[:, :], T.rx3[:, 384:448], A.add))
    V.wait_ge(T.sem.x3b, n3b)
    e = one(V.tensor_tensor(T.q3[:, :], T.rx3[:, 256:320], T.rx3[:, 320:384], A.add))
    w("V", e, e_qg)
    e_yo = ev()
    for v in range(4):
        inc(e_yo, V.tensor_tensor(T.yo[:, v:64:4], T.q3[:, 16 * v:16 * v + 16], T.qg[:, 16 * v:16 * v + 16], A.add))
    e_y = ev()
    for k in range(8):
        qn = "YS"[k % 2]
        n = 65 if k == 7 else 64
        w(qn, e_yo, e_yc)
        inc(e_y, names[qn].dma_start(T.y[:, 64 * k:64 * k + n], T.yo[16 * k:16 * k + 16, 0:n]), 16)
    g.wait_ge(T.sem.l0, m0)
    g.wait_ge(T.sem.l1, m1)
    g.wait_ge(T.sem.l2, m2)
    g.wait_ge(T.sem.l3, m3)
    w("g", e_y)
    for e in range(len(evs)):
        if e not in waited:
            w("g", e)
